import numpy as np
import ml_dtypes


def mxq(x, axis, fmt="e4m3"):
    dtype, down = {"e4m3": (ml_dtypes.float8_e4m3fn, 7), "e5m2": (ml_dtypes.float8_e5m2, 14)}[fmt]
    v = np.moveaxis(np.asarray(x, np.float32).astype(ml_dtypes.bfloat16).astype(np.float64), axis, -1)
    blocks = v.reshape(v.shape[:-1] + (-1, 32))
    amax = np.abs(blocks).max(-1, keepdims=True)
    byte = np.maximum(np.where(amax > 0, np.frexp(amax)[1] - 1 + 127, 0) - down, 1)
    scale = np.exp2(byte - 127.0)
    codes = (blocks / scale).astype(np.float32).astype(dtype).astype(np.float64)
    return np.moveaxis((codes * scale).reshape(v.shape), -1, axis)


WIDE = False


def mx_kscale(k):
    if not WIDE:
        return np.ones(k)
    levels = np.array([24, -24, 12, -12, 0])
    if k % 512:
        return np.exp2(np.random.permutation(np.resize(levels, k // 32))).repeat(32)
    a = np.empty((k // 512, 16))
    for p in range(k // 512):
        a[p, :8] = np.random.permutation(np.resize(levels, 8))
        for g in range(8):
            far = levels[np.abs(levels - a[p, g]) >= 10]
            a[p, g + 8] = far[np.random.randint(len(far))]
    return np.exp2(a.ravel()).repeat(32)


def f64(x):
    return np.asarray(x).astype(np.float64)


def striped8(idx):
    return np.concatenate([v.reshape(-1, 16).T for v in idx]).astype(np.uint16)


def unstriped8(offs):
    return np.stack([offs[16 * g:16 * g + 16].T.reshape(-1) for g in range(8)]).astype(np.int64)


E2M1 = np.array([0.0, 0.5, 1.0, 1.5, 2.0, 3.0, 4.0, 6.0, -0.0, -0.5, -1.0, -1.5, -2.0, -3.0, -4.0, -6.0])


def pack_weight(w, fmt):
    k, n = w.shape
    w = f64(np.asarray(w, np.float32).astype(ml_dtypes.bfloat16)).reshape(k // 32, 32, n)
    amax = np.abs(w).max(1)
    if fmt == "e4m3":
        byte = np.frexp(amax)[1] - 1 + 127 - 7
    else:
        mant, ex = np.frexp(amax / 6.0)
        byte = np.where(mant > 0.5, ex, ex - 1) + 127
    byte = np.clip(np.where(amax > 0, byte, 1), 1, 254)
    scaled = (w * np.exp2(127.0 - byte)[:, None, :]).reshape(k, n).astype(np.float32)
    by_word = np.ascontiguousarray(scaled.reshape(k // 512, 128, 4, n).transpose(0, 1, 3, 2))
    if fmt == "e4m3":
        words = by_word.astype(ml_dtypes.float8_e4m3fn).view(np.uint8)
    else:
        c = by_word.astype(ml_dtypes.float4_e2m1fn).view(np.uint8) & 0xF
        words = (c[..., 0::2] | (c[..., 1::2] << 4)).reshape(k // 512, 128, 2 * n)
    return np.ascontiguousarray(words), np.ascontiguousarray(byte.astype(np.uint8).reshape(k // 512, 16, n))


def unpack_weight(words, scales, fmt):
    g, _, n = scales.shape
    words = np.ascontiguousarray(words).reshape(g, 128, n, -1)
    if fmt == "e4m3":
        vals = words.view(ml_dtypes.float8_e4m3fn).astype(np.float64)
    else:
        nib = np.empty((g, 128, n, 4), np.uint8)
        nib[..., 0::2] = words & 0xF
        nib[..., 1::2] = words >> 4
        vals = E2M1[nib]
    vals = vals * np.repeat(np.exp2(scales.astype(np.float64) - 127.0), 8, axis=1)[..., None]
    return vals.transpose(0, 1, 3, 2).reshape(g * 512, n)


def planes(y):
    n, m = y.shape
    v = y.astype(np.float32).astype(ml_dtypes.bfloat16).astype(np.float64).reshape(n // 32, 32, m)
    top = np.abs(v).max(1)
    byte = np.clip(np.where(top > 0, np.frexp(top)[1] - 1 + 127 - 7, 1), 1, 254)
    codes = (v * np.exp2(127.0 - byte)[:, None, :]).reshape(n, m).astype(np.float32).astype(ml_dtypes.float8_e4m3fn).view(np.uint8)
    words = codes.reshape(n // 512, 128, 4, m).transpose(0, 1, 3, 2)
    return np.ascontiguousarray(words), np.ascontiguousarray(byte.astype(np.uint8).reshape(n // 512, 16, m))


def sigm(f):
    return 1.0 / (1.0 + np.exp(-np.maximum(f, -700.0)))


K, R, N, T, J = 512, 1024, 512, 2048, 1024


def setup_inputs():
    n = np.random.standard_normal
    s = mx_kscale(K)[:, None]
    u = mx_kscale(R)[:, None]
    p_wg = pack_weight(n((K, R)) / np.sqrt(K) / s, "e2m1")
    p_wu = pack_weight(n((K, R)) / np.sqrt(K) / s * u.T, "e2m1")
    return {
        "xT": (n((K, T)) * s).astype(np.float32),
        "wgt": np.repeat(np.random.uniform(0.5, 2.0, (8, J)), 16, axis=0).astype(np.float32),
        "wg_words": p_wg[0],
        "wg_scales": p_wg[1],
        "wu_words": p_wu[0],
        "wu_scales": p_wu[1],
        "wd": (n((R, N)) / np.sqrt(R) / u).astype(np.float32),
        "b": (0.3 * n(N)).astype(np.float32),
        "offs": striped8(np.stack([np.random.permutation(T)[:J] for _ in range(8)])),
    }


def reference(xT, wgt, wg_words, wg_scales, wu_words, wu_scales, wd, b, offs):
    idx = unstriped8(offs)
    rows = np.arange(K)
    xg = f64(wgt)[rows // 4 % 128] * f64(xT)[rows[:, None], idx[rows % 512 // 64]]
    xT_ = mxq(xg, 0, "e4m3")
    wg_ = unpack_weight(wg_words, wg_scales, "e2m1")
    wu_ = unpack_weight(wu_words, wu_scales, "e2m1")
    ga = wg_.T @ xT_
    ub = wu_.T @ xT_
    h = sigm(ga) * ub
    h_ = mxq(h, 0, "e4m3")
    wd_ = mxq(f64(wd), 0, "e4m3")
    y = wd_.T @ h_
    out_0 = y + f64(b)[:, None]
    return (out_0,) + planes(out_0)

@@ -1,0 +1,224 @@
+from contextlib import ExitStack
+
+import concourse.mybir as mybir
+
+K, R, N, T, J = 512, 1024, 512, 2048, 1024
+FLOPS = 2 * K * R * J * 2 + 2 * R * N * J
+
+F32 = mybir.dt.float32
+BF16 = mybir.dt.bfloat16
+I32 = mybir.dt.int32
+U32 = mybir.dt.uint32
+U16 = mybir.dt.uint16
+U8 = mybir.dt.uint8
+FP8X4 = mybir.dt.float8_e4m3fn_x4
+FP4X4 = mybir.dt.float4_e2m1fn_x4
+ACT = mybir.ActivationFunctionType
+MULT = mybir.AluOpType.mult
+
+P = 128
+PACK = 4
+PASSES = R // (P * PACK)
+CHUNK = 256
+CHUNKS = J // CHUNK
+SUB = 128
+PER_COL = 16
+
+
+def tile_list_sigm_biasP_kernel(
+    tc, xT, wgt, wg_words, wg_scales, wu_words, wu_scales, wd, b, offs, out_0, out_1, out_2
+):
+    nc = tc.nc
+    with ExitStack() as ctx:
+        keep = ctx.enter_context(tc.tile_pool(name="keep", bufs=1))
+        ring = ctx.enter_context(tc.tile_pool(name="ring", bufs=3))
+        gate_ps = ctx.enter_context(tc.psum_pool(name="gate_ps", bufs=3))
+        up_ps = ctx.enter_context(tc.psum_pool(name="up_ps", bufs=3))
+        y_ps = ctx.enter_context(tc.psum_pool(name="y_ps", bufs=2))
+
+        offsets = keep.tile([P, J // PER_COL], U16, name="offsets")
+        nc.sync.dma_start(offsets[:], offs)
+
+        raw_scales = keep.tile([P, 2 * R], U8, name="raw_scales")
+        for q in range(4):
+            for w, scales in enumerate((wg_scales, wu_scales)):
+                nc.scalar.dma_start(
+                    raw_scales[32 * q : 32 * q + 4, w * R : (w + 1) * R].bitcast(I32),
+                    scales[0, 4 * q : 4 * q + 4, :].bitcast(I32),
+                )
+        w_scales = keep.tile([P, 2 * R], U8, name="w_scales", align_bytes=64)
+        nc.vector.memset(w_scales[:].bitcast(I32), 0)
+        for q in range(4):
+            rows = slice(32 * q, 32 * q + 4)
+            nc.vector.tensor_copy(
+                w_scales[rows, :].bitcast(I32).rearrange("p (g t q) -> p g q t", t=PACK, q=32),
+                raw_scales[rows, :].bitcast(I32).rearrange("p (g q t) -> p g q t", t=PACK, q=32),
+            )
+
+        warm = keep.tile([P, 8], F32, name="warm")
+        nc.vector.memset(warm[:, 0:1], 0.0)
+        nc.scalar.activation(warm[:, 4:5], warm[:, 0:1], ACT.Sigmoid)
+
+        weight = keep.tile([P, J], F32, name="weight")
+        planes = [keep.tile([P, T], F32, name=f"plane{i}") for i in range(PACK)]
+        x_planes = xT.rearrange("(p i) t -> i p t", i=PACK)
+        half = J // 2
+        nc.sync.dma_start(weight[:, :half], wgt[:, :half])
+        nc.sync.dma_start(planes[0][:], x_planes[0])
+        nc.sync.dma_start(weight[:, half:], wgt[:, half:])
+        for i in range(1, PACK):
+            nc.sync.dma_start(planes[i][:], x_planes[i])
+
+        raw_words = [keep.tile([P, 2 * R], U8, name=f"raw_words{w}") for w in range(2)]
+        for w, words in enumerate((wg_words, wu_words)):
+            nc.sync.dma_start(raw_words[w][:].bitcast(I32), words[0].bitcast(I32))
+
+        bias = keep.tile([P, PACK], F32, name="bias")
+        nc.scalar.dma_start(bias[:], b.rearrange("(p t) -> p t", t=PACK))
+
+        wd_raw = [keep.tile([P, PACK, N], F32, name=f"wd_raw{a}", tag=f"wd_raw{a}", align_bytes=64) for a in range(PASSES)]
+        wd_rows = wd.rearrange("(a q t e) n -> a e q t n", a=PASSES, t=PACK, e=4)
+        for a in range(PASSES):
+            for e in range(4):
+                nc.sync.dma_start(wd_raw[a][e:P:4, :, :], wd_rows[a, e])
+
+        low = keep.tile([P, 2, J], F32, name="low")
+        high = [keep.tile([P, 2, CHUNK], F32, name=f"high{c}") for c in range(CHUNKS)]
+        x_bf = [keep.tile([P, CHUNK, PACK], BF16, name=f"x_bf{c}", align_bytes=64) for c in range(CHUNKS)]
+        x_codes = keep.tile([P, J], U32, name="x_codes", align_bytes=64)
+        x_scales = keep.tile([P, J], U8, name="x_scales", align_bytes=64)
+
+        def gather(out, i, j0, j1):
+            nc.vector.tensor_tensor(
+                out, planes[i][:].indirect(offsets[:, j0 // PER_COL : j1 // PER_COL]), weight[:, j0:j1], MULT
+            )
+
+        def weave_pair(c, pair, src):
+            nc.scalar.copy(
+                x_bf[c][:, :, 2 * pair : 2 * pair + 2],
+                src.rearrange("p t j -> p j t"),
+            )
+
+        for i in range(2):
+            for j0 in range(0, J, half):
+                gather(low[:, i, j0 : j0 + half], i, j0, j0 + half)
+        for c in range(CHUNKS):
+            weave_pair(c, 0, low[:, :, c * CHUNK : (c + 1) * CHUNK])
+        for c in range(CHUNKS):
+            gather(high[c][:, 0, :], 2, c * CHUNK, (c + 1) * CHUNK)
+
+        def finish_x(c):
+            cols = slice(c * CHUNK, (c + 1) * CHUNK)
+            gather(high[c][:, 1, :], 3, c * CHUNK, (c + 1) * CHUNK)
+            weave_pair(c, 1, high[c][:])
+            nc.vector.quantize_mx(
+                out=x_codes[:, cols].bitcast(FP8X4),
+                scales=x_scales[:, cols],
+                in_=x_bf[c][:].rearrange("p j t -> p (j t)"),
+            )
+
+        finish_x(0)
+        finish_x(1)
+
+        w_words = [keep.tile([P, 2 * R], U8, name=f"w_words{w}", align_bytes=64) for w in range(2)]
+        for w in range(2):
+            nc.vector.tensor_copy(
+                w_words[w][:].bitcast(I32).rearrange("p (a t q h) -> p a q t h", t=PACK, q=32, h=2),
+                raw_words[w][:].bitcast(I32).rearrange("p (a q t h) -> p a q t h", t=PACK, q=32, h=2),
+            )
+
+        wd_codes = [keep.tile([P, N], U32, name=f"wd_codes{a}", align_bytes=64) for a in range(PASSES)]
+        wd_scales = [keep.tile([P, N], U8, name=f"wd_scales{a}", align_bytes=64) for a in range(PASSES)]
+
+        def quantize_wd(a):
+            wd_bf = keep.tile([P, N * PACK], BF16, name=f"wd_bf{a}", align_bytes=64)
+            dst = wd_bf[:].rearrange("p (u m t) -> p m t u", u=PACK, t=PACK)
+            src = wd_raw[a][:].rearrange("p t (m u) -> p m t u", u=PACK)
+            if a == 0:
+                nc.scalar.copy(dst, src)
+            else:
+                nc.vector.tensor_copy(dst, src)
+            nc.vector.quantize_mx(out=wd_codes[a][:].bitcast(FP8X4), scales=wd_scales[a][:], in_=wd_bf[:])
+
+        def hidden(c, a):
+            if (c, a) == (1, 0):
+                h_bf = keep.tile([P, CHUNK, PACK], BF16, name="h_bf_on_wd", tag="wd_raw1", align_bytes=64)
+            else:
+                h_bf = ring.tile([P, CHUNK, PACK], BF16, name="h_bf", align_bytes=64)
+            for s in range(CHUNK // SUB):
+                cols = slice(c * CHUNK + s * SUB, c * CHUNK + (s + 1) * SUB)
+                sums = (gate_ps.tile([P, PACK, SUB], F32, name="gate"), up_ps.tile([P, PACK, SUB], F32, name="up"))
+                for w in range(2):
+                    for t in range(PACK):
+                        r0 = (a * PACK + t) * P
+                        nc.tensor.matmul_mx(
+                            out=sums[w][:, t, :],
+                            lhsT=w_words[w][:, 2 * r0 : 2 * (r0 + P)].bitcast(FP4X4),
+                            lhsT_scale=w_scales[:, w * R + r0 : w * R + r0 + P],
+                            rhs=x_codes[:, cols].bitcast(FP8X4),
+                            rhs_scale=x_scales[:, cols],
+                            start=True,
+                            stop=True,
+                        )
+                if (c, a, s) == (1, 0, 0):
+                    sig = keep.tile([P, SUB, PACK], F32, name="sig_on_wd", tag="wd_raw0", align_bytes=64)
+                else:
+                    sig = ring.tile([P, SUB, PACK], F32, name="sig")
+                nc.scalar.activation(sig[:], sums[0][:].rearrange("p t j -> p j t"), ACT.Sigmoid)
+                nc.vector.tensor_tensor(
+                    h_bf[:, s * SUB : (s + 1) * SUB, :], sums[1][:].rearrange("p t j -> p j t"), sig[:], MULT
+                )
+            h_codes = keep.tile([P, CHUNK], U32, name=f"h_codes{c}_{a}", align_bytes=64)
+            h_scales = keep.tile([P, CHUNK], U8, name=f"h_scales{c}_{a}", align_bytes=64)
+            nc.vector.quantize_mx(
+                out=h_codes[:].bitcast(FP8X4), scales=h_scales[:], in_=h_bf[:].rearrange("p j t -> p (j t)")
+            )
+            return h_codes, h_scales
+
+        y_scales = keep.tile([P, J], U8, name="y_scales", align_bytes=64)
+        y_rows = out_0.rearrange("(p u) j -> p u j", u=PACK)
+        y_words = out_1[0].rearrange("p j i -> p (j i)").bitcast(I32)
+
+        def down(c, h):
+            cols = slice(c * CHUNK, (c + 1) * CHUNK)
+            banks = [y_ps.tile([P, 2, CHUNK], F32, name="y_sum") for k in range(2)]
+            for a in range(PASSES):
+                for u in range(PACK):
+                    nc.tensor.matmul_mx(
+                        out=banks[u // 2][:, u % 2, :],
+                        lhsT=wd_codes[a][:, u * P : (u + 1) * P].bitcast(FP8X4),
+                        lhsT_scale=wd_scales[a][:, u * P : (u + 1) * P],
+                        rhs=h[a][0][:].bitcast(FP8X4),
+                        rhs_scale=h[a][1][:],
+                        start=(a == 0 and u % 2 == 0),
+                        stop=(a == PASSES - 1 and u % 2 == 1),
+                    )
+            y = keep.tile([P, PACK, CHUNK], F32, name=f"y{c}")
+            for u in range(PACK):
+                nc.scalar.activation(y[:, u, :], banks[u // 2][:, u % 2, :], ACT.Identity, bias=bias[:, u : u + 1])
+            nc.sync.dma_start(y_rows[:, :, cols], y[:])
+            y_bf = ring.tile([P, CHUNK * PACK], BF16, name="y_bf", align_bytes=64)
+            nc.vector.tensor_copy(
+                y_bf[:].rearrange("p (g i u) -> p g u i", i=4, u=PACK),
+                y[:].rearrange("p u (g i) -> p g u i", i=4),
+            )
+            y_codes = keep.tile([P, CHUNK], U32, name=f"y_codes{c}", align_bytes=64)
+            nc.vector.quantize_mx(out=y_codes[:].bitcast(FP8X4), scales=y_scales[:, cols], in_=y_bf[:])
+            nc.sync.dma_start(y_words[:, cols], y_codes[:].bitcast(I32))
+
+        h = {}
+        for c in range(CHUNKS):
+            if c == 1:
+                quantize_wd(1)
+                quantize_wd(0)
+            for a in range(PASSES):
+                h[c, a] = hidden(c, a)
+                if c == 0:
+                    finish_x(2 + a)
+                if c >= 1 and a == 0:
+                    down(c - 1, [h[c - 1, 0], h[c - 1, 1]])
+        down(CHUNKS - 1, [h[CHUNKS - 1, 0], h[CHUNKS - 1, 1]])
+
+        for q in range(4):
+            queue = nc.sync if q % 2 == 0 else nc.scalar
+            queue.dma_start(out_2[0, 4 * q : 4 * q + 4, :].bitcast(I32), y_scales[32 * q : 32 * q + 4, :].bitcast(I32))

@@ -15,6 +15,7 @@ FP8X4 = mybir.dt.float8_e4m3fn_x4
 FP4X4 = mybir.dt.float4_e2m1fn_x4
 ACT = mybir.ActivationFunctionType
 MULT = mybir.AluOpType.mult
+ADD = mybir.AluOpType.add
 
 P = 128
 PACK = 4
@@ -23,6 +24,11 @@ CHUNK = 256
 CHUNKS = J // CHUNK
 SUB = 128
 PER_COL = 16
+DEPTH = 3
+ON_VECTOR = (2, 2)
+HOLD = (1, 5)
+DOWN_AT = (10, 12)
+CAST_ON_SCALAR = ()
 
 
 def tile_list_sigm_biasP_kernel(
@@ -31,30 +37,24 @@ def tile_list_sigm_biasP_kernel(
     nc = tc.nc
     with ExitStack() as ctx:
         keep = ctx.enter_context(tc.tile_pool(name="keep", bufs=1))
-        ring = ctx.enter_context(tc.tile_pool(name="ring", bufs=3))
-        gate_ps = ctx.enter_context(tc.psum_pool(name="gate_ps", bufs=3))
-        up_ps = ctx.enter_context(tc.psum_pool(name="up_ps", bufs=3))
-        y_ps = ctx.enter_context(tc.psum_pool(name="y_ps", bufs=2))
+        psum = ctx.enter_context(tc.psum_pool(name="psum", bufs=1))
+        gate_banks = [psum.tile([P, PACK, SUB], F32, name=f"gate{k}") for k in range(DEPTH)]
+        up_banks = [psum.tile([P, PACK, SUB], F32, name=f"up{k}") for k in range(DEPTH)]
+        banks = [psum.tile([P, 2, CHUNK], F32, name=f"y_sum{k}") for k in range(2)]
+        sigs = [keep.tile([P, SUB, PACK], F32, name=f"sig{k}") for k in range(DEPTH)]
+        h_bfs = [keep.tile([P, CHUNK, PACK], BF16, name=f"h_bf{k}", align_bytes=64) for k in range(2)]
 
         offsets = keep.tile([P, J // PER_COL], U16, name="offsets")
         nc.sync.dma_start(offsets[:], offs)
 
         raw_scales = keep.tile([P, 2 * R], U8, name="raw_scales")
+        nc.vector.memset(raw_scales[:].bitcast(I32), 0)
         for q in range(4):
             for w, scales in enumerate((wg_scales, wu_scales)):
                 nc.scalar.dma_start(
                     raw_scales[32 * q : 32 * q + 4, w * R : (w + 1) * R].bitcast(I32),
                     scales[0, 4 * q : 4 * q + 4, :].bitcast(I32),
                 )
-        w_scales = keep.tile([P, 2 * R], U8, name="w_scales", align_bytes=64)
-        nc.vector.memset(w_scales[:].bitcast(I32), 0)
-        for q in range(4):
-            rows = slice(32 * q, 32 * q + 4)
-            nc.vector.tensor_copy(
-                w_scales[rows, :].bitcast(I32).rearrange("p (g t q) -> p g q t", t=PACK, q=32),
-                raw_scales[rows, :].bitcast(I32).rearrange("p (g q t) -> p g q t", t=PACK, q=32),
-            )
-
         warm = keep.tile([P, 8], F32, name="warm")
         nc.vector.memset(warm[:, 0:1], 0.0)
         nc.scalar.activation(warm[:, 4:5], warm[:, 0:1], ACT.Sigmoid)
@@ -74,16 +74,16 @@ def tile_list_sigm_biasP_kernel(
             nc.sync.dma_start(raw_words[w][:].bitcast(I32), words[0].bitcast(I32))
 
         bias = keep.tile([P, PACK], F32, name="bias")
-        nc.scalar.dma_start(bias[:], b.rearrange("(p t) -> p t", t=PACK))
+        nc.gpsimd.dma_start(bias[:], b.rearrange("(p t) -> p t", t=PACK))
 
-        wd_raw = [keep.tile([P, PACK, N], F32, name=f"wd_raw{a}", tag=f"wd_raw{a}", align_bytes=64) for a in range(PASSES)]
+        wd_raw = [keep.tile([P, PACK, 2 * N], F32, name=f"wd_raw{a}") for a in range(PASSES)]
         wd_rows = wd.rearrange("(a q t e) n -> a e q t n", a=PASSES, t=PACK, e=4)
         for a in range(PASSES):
             for e in range(4):
-                nc.sync.dma_start(wd_raw[a][e:P:4, :, :], wd_rows[a, e])
+                nc.sync.dma_start(wd_raw[a][e:P:4, :, N:], wd_rows[a, e])
 
         low = keep.tile([P, 2, J], F32, name="low")
-        high = [keep.tile([P, 2, CHUNK], F32, name=f"high{c}") for c in range(CHUNKS)]
+        high = keep.tile([P, CHUNKS + 2, CHUNK], F32, name="high")
         x_bf = [keep.tile([P, CHUNK, PACK], BF16, name=f"x_bf{c}", align_bytes=64) for c in range(CHUNKS)]
         x_codes = keep.tile([P, J], U32, name="x_codes", align_bytes=64)
         x_scales = keep.tile([P, J], U8, name="x_scales", align_bytes=64)
@@ -102,15 +102,21 @@ def tile_list_sigm_biasP_kernel(
         for i in range(2):
             for j0 in range(0, J, half):
                 gather(low[:, i, j0 : j0 + half], i, j0, j0 + half)
+        w_scales = keep.tile([P, 2 * R], U8, name="w_scales", align_bytes=64)
+        nc.vector.tensor_copy(
+            w_scales[:].bitcast(I32).rearrange("p (g t q) -> p g q t", t=PACK, q=32),
+            raw_scales[:].bitcast(I32).rearrange("p (g q t) -> p g q t", t=PACK, q=32),
+        )
         for c in range(CHUNKS):
             weave_pair(c, 0, low[:, :, c * CHUNK : (c + 1) * CHUNK])
         for c in range(CHUNKS):
-            gather(high[c][:, 0, :], 2, c * CHUNK, (c + 1) * CHUNK)
+            gather(high[:, c, :], 2, c * CHUNK, (c + 1) * CHUNK)
 
         def finish_x(c):
             cols = slice(c * CHUNK, (c + 1) * CHUNK)
-            gather(high[c][:, 1, :], 3, c * CHUNK, (c + 1) * CHUNK)
-            weave_pair(c, 1, high[c][:])
+            row = CHUNKS + c % 2
+            gather(high[:, row, :], 3, c * CHUNK, (c + 1) * CHUNK)
+            weave_pair(c, 1, high[:, c : row + 1 : row - c, :])
             nc.vector.quantize_mx(
                 out=x_codes[:, cols].bitcast(FP8X4),
                 scales=x_scales[:, cols],
@@ -130,94 +136,124 @@ def tile_list_sigm_biasP_kernel(
         wd_codes = [keep.tile([P, N], U32, name=f"wd_codes{a}", align_bytes=64) for a in range(PASSES)]
         wd_scales = [keep.tile([P, N], U8, name=f"wd_scales{a}", align_bytes=64) for a in range(PASSES)]
 
-        def quantize_wd(a):
-            wd_bf = keep.tile([P, N * PACK], BF16, name=f"wd_bf{a}", align_bytes=64)
-            dst = wd_bf[:].rearrange("p (u m t) -> p m t u", u=PACK, t=PACK)
-            src = wd_raw[a][:].rearrange("p t (m u) -> p m t u", u=PACK)
-            if a == 0:
-                nc.scalar.copy(dst, src)
-            else:
-                nc.vector.tensor_copy(dst, src)
-            nc.vector.quantize_mx(out=wd_codes[a][:].bitcast(FP8X4), scales=wd_scales[a][:], in_=wd_bf[:])
+        wd_bf = [keep.tile([P, N * PACK], BF16, name=f"wd_bf{a}", align_bytes=64) for a in range(PASSES)]
 
-        def hidden(c, a):
-            if (c, a) == (1, 0):
-                h_bf = keep.tile([P, CHUNK, PACK], BF16, name="h_bf_on_wd", tag="wd_raw1", align_bytes=64)
+        def weave_wd(a, k):
+            dst = wd_bf[a][:].rearrange("p (u m t) -> p m t u", u=PACK, t=PACK)[:, 32 * k : 32 * (k + 1)]
+            src = wd_raw[a][:, :, N + P * k : N + P * (k + 1)].rearrange("p t (m u) -> p m t u", u=PACK)
+            if k >= PACK - ON_VECTOR[a]:
+                nc.vector.tensor_copy(dst, src)
             else:
-                h_bf = ring.tile([P, CHUNK, PACK], BF16, name="h_bf", align_bytes=64)
-            for s in range(CHUNK // SUB):
-                cols = slice(c * CHUNK + s * SUB, c * CHUNK + (s + 1) * SUB)
-                sums = (gate_ps.tile([P, PACK, SUB], F32, name="gate"), up_ps.tile([P, PACK, SUB], F32, name="up"))
-                for w in range(2):
-                    for t in range(PACK):
-                        r0 = (a * PACK + t) * P
-                        nc.tensor.matmul_mx(
-                            out=sums[w][:, t, :],
-                            lhsT=w_words[w][:, 2 * r0 : 2 * (r0 + P)].bitcast(FP4X4),
-                            lhsT_scale=w_scales[:, w * R + r0 : w * R + r0 + P],
-                            rhs=x_codes[:, cols].bitcast(FP8X4),
-                            rhs_scale=x_scales[:, cols],
-                            start=True,
-                            stop=True,
-                        )
-                if (c, a, s) == (1, 0, 0):
-                    sig = keep.tile([P, SUB, PACK], F32, name="sig_on_wd", tag="wd_raw0", align_bytes=64)
-                else:
-                    sig = ring.tile([P, SUB, PACK], F32, name="sig")
-                nc.scalar.activation(sig[:], sums[0][:].rearrange("p t j -> p j t"), ACT.Sigmoid)
-                nc.vector.tensor_tensor(
-                    h_bf[:, s * SUB : (s + 1) * SUB, :], sums[1][:].rearrange("p t j -> p j t"), sig[:], MULT
-                )
-            h_codes = keep.tile([P, CHUNK], U32, name=f"h_codes{c}_{a}", align_bytes=64)
-            h_scales = keep.tile([P, CHUNK], U8, name=f"h_scales{c}_{a}", align_bytes=64)
+                nc.scalar.copy(dst, src)
+            if k == PACK - 1:
+                nc.vector.quantize_mx(out=wd_codes[a][:].bitcast(FP8X4), scales=wd_scales[a][:], in_=wd_bf[a][:])
+
+        h_codes = [keep.tile([P, J], U32, name=f"h_codes{a}", align_bytes=64) for a in range(PASSES)]
+        h_scales = [keep.tile([P, J], U8, name=f"h_scales{a}", align_bytes=64) for a in range(PASSES)]
+
+        def hidden(unit, a, j0, h_bf):
+            cols = slice(j0, j0 + SUB)
+            sums = (gate_banks[unit % DEPTH], up_banks[unit % DEPTH])
+            for w in range(2):
+                for t in range(PACK):
+                    r0 = (a * PACK + t) * P
+                    nc.tensor.matmul_mx(
+                        out=sums[w][:, t, :],
+                        lhsT=w_words[w][:, 2 * r0 : 2 * (r0 + P)].bitcast(FP4X4),
+                        lhsT_scale=w_scales[:, w * R + r0 : w * R + r0 + P],
+                        rhs=x_codes[:, cols].bitcast(FP8X4),
+                        rhs_scale=x_scales[:, cols],
+                        start=True,
+                        stop=True,
+                    )
+            sig = sigs[unit % DEPTH][:]
+            for b2 in range(PASSES):
+                k = unit - HOLD[b2]
+                if 0 <= k < PACK:
+                    sig = wd_raw[b2][:, k, P * (k + 1) : P * (k + 1) + N].rearrange("p (j t) -> p j t", t=PACK)
+            nc.scalar.activation(sig, sums[0][:].rearrange("p t j -> p j t"), ACT.Sigmoid)
+            nc.vector.tensor_tensor(h_bf, sums[1][:].rearrange("p t j -> p j t"), sig, MULT)
+
+        def quantize_h(a, cols, h_bf):
             nc.vector.quantize_mx(
-                out=h_codes[:].bitcast(FP8X4), scales=h_scales[:], in_=h_bf[:].rearrange("p j t -> p (j t)")
+                out=h_codes[a][:, cols].bitcast(FP8X4), scales=h_scales[a][:, cols], in_=h_bf.rearrange("p j t -> p (j t)")
             )
-            return h_codes, h_scales
 
         y_scales = keep.tile([P, J], U8, name="y_scales", align_bytes=64)
         y_rows = out_0.rearrange("(p u) j -> p u j", u=PACK)
         y_words = out_1[0].rearrange("p j i -> p (j i)").bitcast(I32)
 
-        def down(c, h):
-            cols = slice(c * CHUNK, (c + 1) * CHUNK)
-            banks = [y_ps.tile([P, 2, CHUNK], F32, name="y_sum") for k in range(2)]
+        def down(j0, width, share):
+            cols = slice(j0, j0 + width)
             for a in range(PASSES):
                 for u in range(PACK):
                     nc.tensor.matmul_mx(
-                        out=banks[u // 2][:, u % 2, :],
+                        out=banks[u // 2][:, u % 2, :width],
                         lhsT=wd_codes[a][:, u * P : (u + 1) * P].bitcast(FP8X4),
                         lhsT_scale=wd_scales[a][:, u * P : (u + 1) * P],
-                        rhs=h[a][0][:].bitcast(FP8X4),
-                        rhs_scale=h[a][1][:],
+                        rhs=h_codes[a][:, cols].bitcast(FP8X4),
+                        rhs_scale=h_scales[a][:, cols],
                         start=(a == 0 and u % 2 == 0),
                         stop=(a == PASSES - 1 and u % 2 == 1),
                     )
-            y = keep.tile([P, PACK, CHUNK], F32, name=f"y{c}")
+            y = keep.tile([P, PACK, width], F32, name=f"y{j0}")
             for u in range(PACK):
-                nc.scalar.activation(y[:, u, :], banks[u // 2][:, u % 2, :], ACT.Identity, bias=bias[:, u : u + 1])
+                if share and u >= 2:
+                    nc.vector.tensor_scalar(y[:, u, :], banks[1][:, u % 2, :width], bias[:, u : u + 1], None, ADD)
+                else:
+                    nc.scalar.activation(
+                        y[:, u, :], banks[u // 2][:, u % 2, :width], ACT.Identity, bias=bias[:, u : u + 1]
+                    )
             nc.sync.dma_start(y_rows[:, :, cols], y[:])
-            y_bf = ring.tile([P, CHUNK * PACK], BF16, name="y_bf", align_bytes=64)
-            nc.vector.tensor_copy(
+            return y
+
+        def planes_of(j0, width, y):
+            cols = slice(j0, j0 + width)
+            y_bf = keep.tile([P, width * PACK], BF16, name=f"y_bf{j0}", align_bytes=64)
+            cast = nc.scalar.copy if j0 in CAST_ON_SCALAR else nc.vector.tensor_copy
+            cast(
                 y_bf[:].rearrange("p (g i u) -> p g u i", i=4, u=PACK),
                 y[:].rearrange("p u (g i) -> p g u i", i=4),
             )
-            y_codes = keep.tile([P, CHUNK], U32, name=f"y_codes{c}", align_bytes=64)
+            y_codes = keep.tile([P, width], U32, name=f"y_codes{j0}", align_bytes=64)
             nc.vector.quantize_mx(out=y_codes[:].bitcast(FP8X4), scales=y_scales[:, cols], in_=y_bf[:])
             nc.sync.dma_start(y_words[:, cols], y_codes[:].bitcast(I32))
 
-        h = {}
-        for c in range(CHUNKS):
-            if c == 1:
-                quantize_wd(1)
-                quantize_wd(0)
+        unit = 0
+        ys = {}
+        for c in range(CHUNKS - 1):
             for a in range(PASSES):
-                h[c, a] = hidden(c, a)
+                for s in range(2):
+                    for b2 in range(PASSES):
+                        if 0 <= unit - HOLD[b2] < PACK:
+                            weave_wd(b2, unit - HOLD[b2])
+                    hidden(unit, a, c * CHUNK + s * SUB, h_bfs[a][:, s * SUB : (s + 1) * SUB, :])
+                    unit = unit + 1
+                quantize_h(a, slice(c * CHUNK, (c + 1) * CHUNK), h_bfs[a][:])
                 if c == 0:
                     finish_x(2 + a)
-                if c >= 1 and a == 0:
-                    down(c - 1, [h[c - 1, 0], h[c - 1, 1]])
-        down(CHUNKS - 1, [h[CHUNKS - 1, 0], h[CHUNKS - 1, 1]])
+                for d in range(2):
+                    if unit == DOWN_AT[d]:
+                        ys[d] = down(d * CHUNK, CHUNK, False)
+                    if unit == DOWN_AT[d] + 2:
+                        planes_of(d * CHUNK, CHUNK, ys[d])
+        last = (CHUNKS - 1) * CHUNK
+        for d in range(2):
+            if DOWN_AT[d] + 2 > unit:
+                planes_of(d * CHUNK, CHUNK, ys[d])
+        for s in range(2):
+            for a in range(PASSES):
+                hidden(unit, a, last + s * SUB, h_bfs[a][:, s * SUB : (s + 1) * SUB, :])
+                unit = unit + 1
+                quantize_h(a, slice(last + s * SUB, last + (s + 1) * SUB), h_bfs[a][:, s * SUB : (s + 1) * SUB, :])
+                if (s, a) == (0, 0):
+                    ys[2] = down(last - CHUNK, CHUNK, False)
+                if (s, a) == (1, 0):
+                    ys[3] = down(last, SUB, False)
+                    planes_of(last - CHUNK, CHUNK, ys[2])
+        ys[4] = down(last + SUB, SUB, True)
+        planes_of(last, SUB, ys[3])
+        planes_of(last + SUB, SUB, ys[4])
 
         for q in range(4):
             queue = nc.sync if q % 2 == 0 else nc.scalar

@@ -25,10 +25,8 @@ CHUNKS = J // CHUNK
 SUB = 128
 PER_COL = 16
 DEPTH = 3
-ON_VECTOR = (2, 2)
-HOLD = (1, 5)
-DOWN_AT = (10, 12)
-CAST_ON_SCALAR = ()
+ON_SCALAR = (1, 2)
+WD_AT = (1, 2, 3, 4, 4, 5, 5, 6)
 
 
 def tile_list_sigm_biasP_kernel(
@@ -40,32 +38,35 @@ def tile_list_sigm_biasP_kernel(
         psum = ctx.enter_context(tc.psum_pool(name="psum", bufs=1))
         gate_banks = [psum.tile([P, PACK, SUB], F32, name=f"gate{k}") for k in range(DEPTH)]
         up_banks = [psum.tile([P, PACK, SUB], F32, name=f"up{k}") for k in range(DEPTH)]
-        banks = [psum.tile([P, 2, CHUNK], F32, name=f"y_sum{k}") for k in range(2)]
+        y_banks = [psum.tile([P, 2, CHUNK], F32, name=f"y_sum{k}") for k in range(2)]
         sigs = [keep.tile([P, SUB, PACK], F32, name=f"sig{k}") for k in range(DEPTH)]
-        h_bfs = [keep.tile([P, CHUNK, PACK], BF16, name=f"h_bf{k}", align_bytes=64) for k in range(2)]
+        h_bfs = [keep.tile([P, CHUNK, PACK], BF16, name=f"h_bf{k}", align_bytes=64) for k in range(PASSES)]
 
         offsets = keep.tile([P, J // PER_COL], U16, name="offsets")
         nc.sync.dma_start(offsets[:], offs)
 
-        raw_scales = keep.tile([P, 2 * R], U8, name="raw_scales")
-        nc.vector.memset(raw_scales[:].bitcast(I32), 0)
-        for q in range(4):
-            for w, scales in enumerate((wg_scales, wu_scales)):
-                nc.scalar.dma_start(
-                    raw_scales[32 * q : 32 * q + 4, w * R : (w + 1) * R].bitcast(I32),
-                    scales[0, 4 * q : 4 * q + 4, :].bitcast(I32),
-                )
+        raw_scales = [keep.tile([P, R], U8, name=f"raw_scales{w}") for w in range(2)]
         warm = keep.tile([P, 8], F32, name="warm")
+
+        def load_scales(w, scales):
+            nc.vector.memset(raw_scales[w][:].bitcast(I32), 0)
+            for q in range(4):
+                nc.scalar.dma_start(
+                    raw_scales[w][32 * q : 32 * q + 4, :].bitcast(I32), scales[0, 4 * q : 4 * q + 4, :].bitcast(I32)
+                )
+
+        load_scales(0, wg_scales)
         nc.vector.memset(warm[:, 0:1], 0.0)
         nc.scalar.activation(warm[:, 4:5], warm[:, 0:1], ACT.Sigmoid)
+        load_scales(1, wu_scales)
 
-        weight = keep.tile([P, J], F32, name="weight")
-        planes = [keep.tile([P, T], F32, name=f"plane{i}") for i in range(PACK)]
-        x_planes = xT.rearrange("(p i) t -> i p t", i=PACK)
         half = J // 2
-        nc.sync.dma_start(weight[:, :half], wgt[:, :half])
+        weights = [keep.tile([P, half], F32, name=f"weight{i}") for i in range(2)]
+        planes = [keep.tile([P, T], F32, name=f"plane{i}", align_bytes=64) for i in range(PACK)]
+        x_planes = xT.rearrange("(p i) t -> i p t", i=PACK)
+        nc.sync.dma_start(weights[0][:], wgt[:, :half])
         nc.sync.dma_start(planes[0][:], x_planes[0])
-        nc.sync.dma_start(weight[:, half:], wgt[:, half:])
+        nc.sync.dma_start(weights[1][:], wgt[:, half:])
         for i in range(1, PACK):
             nc.sync.dma_start(planes[i][:], x_planes[i])
 
@@ -73,86 +74,94 @@ def tile_list_sigm_biasP_kernel(
         for w, words in enumerate((wg_words, wu_words)):
             nc.sync.dma_start(raw_words[w][:].bitcast(I32), words[0].bitcast(I32))
 
-        bias = keep.tile([P, PACK], F32, name="bias")
-        nc.gpsimd.dma_start(bias[:], b.rearrange("(p t) -> p t", t=PACK))
-
-        wd_raw = [keep.tile([P, PACK, 2 * N], F32, name=f"wd_raw{a}") for a in range(PASSES)]
-        wd_rows = wd.rearrange("(a q t e) n -> a e q t n", a=PASSES, t=PACK, e=4)
+        wd_raw = [keep.tile([P, PACK, N], F32, name=f"wd_raw{a}") for a in range(PASSES)]
+        wd_rows = wd.rearrange("(a q t e) n -> a t q e n", a=PASSES, t=PACK, e=4)
         for a in range(PASSES):
-            for e in range(4):
-                nc.sync.dma_start(wd_raw[a][e:P:4, :, N:], wd_rows[a, e])
+            for t in range(PACK):
+                nc.sync.dma_start(wd_raw[a][:, t, :], wd_rows[a, t])
+        bias = keep.tile([P, PACK], F32, name="bias")
+        nc.sync.dma_start(bias[:], b.rearrange("(p t) -> p t", t=PACK))
 
         low = keep.tile([P, 2, J], F32, name="low")
         high = keep.tile([P, CHUNKS + 2, CHUNK], F32, name="high")
         x_bf = [keep.tile([P, CHUNK, PACK], BF16, name=f"x_bf{c}", align_bytes=64) for c in range(CHUNKS)]
-        x_codes = keep.tile([P, J], U32, name="x_codes", align_bytes=64)
-        x_scales = keep.tile([P, J], U8, name="x_scales", align_bytes=64)
+        x_codes = [keep.tile([P, CHUNK], U32, name=f"x_codes{c}", align_bytes=64) for c in range(CHUNKS)]
+        x_scales = [keep.tile([P, CHUNK], U8, name=f"x_scales{c}", align_bytes=64) for c in range(CHUNKS)]
 
         def gather(out, i, j0, j1):
             nc.vector.tensor_tensor(
-                out, planes[i][:].indirect(offsets[:, j0 // PER_COL : j1 // PER_COL]), weight[:, j0:j1], MULT
+                out,
+                planes[i][:].indirect(offsets[:, j0 // PER_COL : j1 // PER_COL]),
+                weights[j0 // half][:, j0 % half : j0 % half + j1 - j0],
+                MULT,
             )
 
         def weave_pair(c, pair, src):
-            nc.scalar.copy(
-                x_bf[c][:, :, 2 * pair : 2 * pair + 2],
-                src.rearrange("p t j -> p j t"),
+            nc.scalar.copy(x_bf[c][:, :, 2 * pair : 2 * pair + 2], src.rearrange("p t j -> p j t"))
+
+        w_scales = []
+
+        def deal_scales(w):
+            w_scales.append(keep.tile([P, R], U8, name=f"w_scales{w}", tag=f"plane{2 * w}", align_bytes=64))
+            nc.vector.tensor_copy(
+                w_scales[w][:].bitcast(I32).rearrange("p (g t q) -> p g q t", t=PACK, q=32),
+                raw_scales[w][:].bitcast(I32).rearrange("p (g q t) -> p g q t", t=PACK, q=32),
             )
 
         for i in range(2):
             for j0 in range(0, J, half):
                 gather(low[:, i, j0 : j0 + half], i, j0, j0 + half)
-        w_scales = keep.tile([P, 2 * R], U8, name="w_scales", align_bytes=64)
-        nc.vector.tensor_copy(
-            w_scales[:].bitcast(I32).rearrange("p (g t q) -> p g q t", t=PACK, q=32),
-            raw_scales[:].bitcast(I32).rearrange("p (g q t) -> p g q t", t=PACK, q=32),
-        )
+            if i == 0:
+                deal_scales(0)
         for c in range(CHUNKS):
             weave_pair(c, 0, low[:, :, c * CHUNK : (c + 1) * CHUNK])
-        for c in range(CHUNKS):
-            gather(high[:, c, :], 2, c * CHUNK, (c + 1) * CHUNK)
+        for c in range(0, CHUNKS, 2):
+            gather(high[:, c : c + 2, :].rearrange("p c j -> p (c j)"), 2, c * CHUNK, (c + 2) * CHUNK)
+        deal_scales(1)
 
-        def finish_x(c):
-            cols = slice(c * CHUNK, (c + 1) * CHUNK)
+        def last_plane(c):
             row = CHUNKS + c % 2
             gather(high[:, row, :], 3, c * CHUNK, (c + 1) * CHUNK)
             weave_pair(c, 1, high[:, c : row + 1 : row - c, :])
+
+        def quantize_x(c):
             nc.vector.quantize_mx(
-                out=x_codes[:, cols].bitcast(FP8X4),
-                scales=x_scales[:, cols],
-                in_=x_bf[c][:].rearrange("p j t -> p (j t)"),
+                out=x_codes[c][:].bitcast(FP8X4), scales=x_scales[c][:], in_=x_bf[c][:].rearrange("p j t -> p (j t)")
             )
 
-        finish_x(0)
-        finish_x(1)
-
         w_words = [keep.tile([P, 2 * R], U8, name=f"w_words{w}", align_bytes=64) for w in range(2)]
-        for w in range(2):
+
+        def deal_words(w):
             nc.vector.tensor_copy(
                 w_words[w][:].bitcast(I32).rearrange("p (a t q h) -> p a q t h", t=PACK, q=32, h=2),
                 raw_words[w][:].bitcast(I32).rearrange("p (a q t h) -> p a q t h", t=PACK, q=32, h=2),
             )
 
+        last_plane(0)
+        deal_words(0)
+        last_plane(1)
+        quantize_x(0)
+        deal_words(1)
+
         wd_codes = [keep.tile([P, N], U32, name=f"wd_codes{a}", align_bytes=64) for a in range(PASSES)]
         wd_scales = [keep.tile([P, N], U8, name=f"wd_scales{a}", align_bytes=64) for a in range(PASSES)]
-
         wd_bf = [keep.tile([P, N * PACK], BF16, name=f"wd_bf{a}", align_bytes=64) for a in range(PASSES)]
 
         def weave_wd(a, k):
             dst = wd_bf[a][:].rearrange("p (u m t) -> p m t u", u=PACK, t=PACK)[:, 32 * k : 32 * (k + 1)]
-            src = wd_raw[a][:, :, N + P * k : N + P * (k + 1)].rearrange("p t (m u) -> p m t u", u=PACK)
-            if k >= PACK - ON_VECTOR[a]:
-                nc.vector.tensor_copy(dst, src)
-            else:
+            src = wd_raw[a][:, :, P * k : P * (k + 1)].rearrange("p t (m u) -> p m t u", u=PACK)
+            if k >= PACK - ON_SCALAR[a]:
                 nc.scalar.copy(dst, src)
+            else:
+                nc.vector.tensor_copy(dst, src)
             if k == PACK - 1:
                 nc.vector.quantize_mx(out=wd_codes[a][:].bitcast(FP8X4), scales=wd_scales[a][:], in_=wd_bf[a][:])
 
         h_codes = [keep.tile([P, J], U32, name=f"h_codes{a}", align_bytes=64) for a in range(PASSES)]
         h_scales = [keep.tile([P, J], U8, name=f"h_scales{a}", align_bytes=64) for a in range(PASSES)]
 
-        def hidden(unit, a, j0, h_bf):
-            cols = slice(j0, j0 + SUB)
+        def hidden(unit, c, a, s):
+            cols = slice(s * SUB, (s + 1) * SUB)
             sums = (gate_banks[unit % DEPTH], up_banks[unit % DEPTH])
             for w in range(2):
                 for t in range(PACK):
@@ -160,58 +169,57 @@ def tile_list_sigm_biasP_kernel(
                     nc.tensor.matmul_mx(
                         out=sums[w][:, t, :],
                         lhsT=w_words[w][:, 2 * r0 : 2 * (r0 + P)].bitcast(FP4X4),
-                        lhsT_scale=w_scales[:, w * R + r0 : w * R + r0 + P],
-                        rhs=x_codes[:, cols].bitcast(FP8X4),
-                        rhs_scale=x_scales[:, cols],
+                        lhsT_scale=w_scales[w][:, r0 : r0 + P],
+                        rhs=x_codes[c][:, cols].bitcast(FP8X4),
+                        rhs_scale=x_scales[c][:, cols],
                         start=True,
                         stop=True,
                     )
             sig = sigs[unit % DEPTH][:]
-            for b2 in range(PASSES):
-                k = unit - HOLD[b2]
-                if 0 <= k < PACK:
-                    sig = wd_raw[b2][:, k, P * (k + 1) : P * (k + 1) + N].rearrange("p (j t) -> p j t", t=PACK)
             nc.scalar.activation(sig, sums[0][:].rearrange("p t j -> p j t"), ACT.Sigmoid)
-            nc.vector.tensor_tensor(h_bf, sums[1][:].rearrange("p t j -> p j t"), sig, MULT)
+            nc.vector.tensor_tensor(h_bfs[a][:, cols, :], sums[1][:].rearrange("p t j -> p j t"), sig, MULT)
 
-        def quantize_h(a, cols, h_bf):
+        def quantize_h(a, j0, width):
+            s0 = j0 % CHUNK
             nc.vector.quantize_mx(
-                out=h_codes[a][:, cols].bitcast(FP8X4), scales=h_scales[a][:, cols], in_=h_bf.rearrange("p j t -> p (j t)")
+                out=h_codes[a][:, j0 : j0 + width].bitcast(FP8X4),
+                scales=h_scales[a][:, j0 : j0 + width],
+                in_=h_bfs[a][:, s0 : s0 + width, :].rearrange("p j t -> p (j t)"),
             )
 
         y_scales = keep.tile([P, J], U8, name="y_scales", align_bytes=64)
         y_rows = out_0.rearrange("(p u) j -> p u j", u=PACK)
         y_words = out_1[0].rearrange("p j i -> p (j i)").bitcast(I32)
 
-        def down(j0, width, share):
+        def down(j0, width, banks, share):
             cols = slice(j0, j0 + width)
-            for a in range(PASSES):
-                for u in range(PACK):
-                    nc.tensor.matmul_mx(
-                        out=banks[u // 2][:, u % 2, :width],
-                        lhsT=wd_codes[a][:, u * P : (u + 1) * P].bitcast(FP8X4),
-                        lhsT_scale=wd_scales[a][:, u * P : (u + 1) * P],
-                        rhs=h_codes[a][:, cols].bitcast(FP8X4),
-                        rhs_scale=h_scales[a][:, cols],
-                        start=(a == 0 and u % 2 == 0),
-                        stop=(a == PASSES - 1 and u % 2 == 1),
-                    )
             y = keep.tile([P, PACK, width], F32, name=f"y{j0}")
-            for u in range(PACK):
-                if share and u >= 2:
-                    nc.vector.tensor_scalar(y[:, u, :], banks[1][:, u % 2, :width], bias[:, u : u + 1], None, ADD)
-                else:
-                    nc.scalar.activation(
-                        y[:, u, :], banks[u // 2][:, u % 2, :width], ACT.Identity, bias=bias[:, u : u + 1]
-                    )
+            for k, bank in enumerate(banks):
+                for a in range(PASSES):
+                    for v in range(2):
+                        u = 2 * k + v
+                        nc.tensor.matmul_mx(
+                            out=bank[:, v, :],
+                            lhsT=wd_codes[a][:, u * P : (u + 1) * P].bitcast(FP8X4),
+                            lhsT_scale=wd_scales[a][:, u * P : (u + 1) * P],
+                            rhs=h_codes[a][:, cols].bitcast(FP8X4),
+                            rhs_scale=h_scales[a][:, cols],
+                            start=(a == 0 and v == 0),
+                            stop=(a == PASSES - 1 and v == 1),
+                        )
+                for v in range(2):
+                    u = 2 * k + v
+                    if share and k == 1:
+                        nc.vector.tensor_scalar(y[:, u, :], bank[:, v, :], bias[:, u : u + 1], None, ADD)
+                    else:
+                        nc.scalar.activation(y[:, u, :], bank[:, v, :], ACT.Identity, bias=bias[:, u : u + 1])
             nc.sync.dma_start(y_rows[:, :, cols], y[:])
             return y
 
         def planes_of(j0, width, y):
             cols = slice(j0, j0 + width)
             y_bf = keep.tile([P, width * PACK], BF16, name=f"y_bf{j0}", align_bytes=64)
-            cast = nc.scalar.copy if j0 in CAST_ON_SCALAR else nc.vector.tensor_copy
-            cast(
+            nc.vector.tensor_copy(
                 y_bf[:].rearrange("p (g i u) -> p g u i", i=4, u=PACK),
                 y[:].rearrange("p u (g i) -> p g u i", i=4),
             )
@@ -219,41 +227,42 @@ def tile_list_sigm_biasP_kernel(
             nc.vector.quantize_mx(out=y_codes[:].bitcast(FP8X4), scales=y_scales[:, cols], in_=y_bf[:])
             nc.sync.dma_start(y_words[:, cols], y_codes[:].bitcast(I32))
 
-        unit = 0
+        last = CHUNKS - 1
+        units = [(c, a, s) for c in range(last) for a in range(PASSES) for s in range(2)]
+        units = units + [(last, a, s) for s in range(2) for a in range(PASSES)]
         ys = {}
-        for c in range(CHUNKS - 1):
-            for a in range(PASSES):
-                for s in range(2):
-                    for b2 in range(PASSES):
-                        if 0 <= unit - HOLD[b2] < PACK:
-                            weave_wd(b2, unit - HOLD[b2])
-                    hidden(unit, a, c * CHUNK + s * SUB, h_bfs[a][:, s * SUB : (s + 1) * SUB, :])
-                    unit = unit + 1
-                quantize_h(a, slice(c * CHUNK, (c + 1) * CHUNK), h_bfs[a][:])
-                if c == 0:
-                    finish_x(2 + a)
-                for d in range(2):
-                    if unit == DOWN_AT[d]:
-                        ys[d] = down(d * CHUNK, CHUNK, False)
-                    if unit == DOWN_AT[d] + 2:
-                        planes_of(d * CHUNK, CHUNK, ys[d])
-        last = (CHUNKS - 1) * CHUNK
-        for d in range(2):
-            if DOWN_AT[d] + 2 > unit:
-                planes_of(d * CHUNK, CHUNK, ys[d])
-        for s in range(2):
-            for a in range(PASSES):
-                hidden(unit, a, last + s * SUB, h_bfs[a][:, s * SUB : (s + 1) * SUB, :])
-                unit = unit + 1
-                quantize_h(a, slice(last + s * SUB, last + (s + 1) * SUB), h_bfs[a][:, s * SUB : (s + 1) * SUB, :])
-                if (s, a) == (0, 0):
-                    ys[2] = down(last - CHUNK, CHUNK, False)
-                if (s, a) == (1, 0):
-                    ys[3] = down(last, SUB, False)
-                    planes_of(last - CHUNK, CHUNK, ys[2])
-        ys[4] = down(last + SUB, SUB, True)
-        planes_of(last, SUB, ys[3])
-        planes_of(last + SUB, SUB, ys[4])
+        for unit, (c, a, s) in enumerate(units):
+            hidden(unit, c, a, s)
+            if unit < 2:
+                if unit == 0:
+                    quantize_x(1)
+                last_plane(2 + unit)
+            elif unit < 4:
+                quantize_x(unit)
+            for k, at in enumerate(WD_AT):
+                if at == unit:
+                    weave_wd(k // PACK, k % PACK)
+            if unit >= 1:
+                pc, pa, ps = units[unit - 1]
+                if pc == last:
+                    quantize_h(pa, pc * CHUNK + ps * SUB, SUB)
+                elif ps == 1:
+                    quantize_h(pa, pc * CHUNK, CHUNK)
+            for d in range(last):
+                ready = max(4 * d + 4, max(WD_AT))
+                if unit == ready:
+                    ys[d] = down(d * CHUNK, CHUNK, y_banks, False)
+                if unit == ready + 2:
+                    planes_of(d * CHUNK, CHUNK, ys[d])
+            if unit == len(units) - 2:
+                tail = [gate_banks[(unit - 1) % DEPTH][:, 0:2, :], gate_banks[unit % DEPTH][:, 0:2, :]]
+                ys[last] = down(last * CHUNK, SUB, tail, False)
+        unit = len(units) - 1
+        quantize_h(PASSES - 1, J - SUB, SUB)
+        tail = [gate_banks[unit % DEPTH][:, 0:2, :], up_banks[(unit - 2) % DEPTH][:, 0:2, :]]
+        y_end = down(J - SUB, SUB, tail, True)
+        planes_of(last * CHUNK, SUB, ys[last])
+        planes_of(J - SUB, SUB, y_end)
 
         for q in range(4):
             queue = nc.sync if q % 2 == 0 else nc.scalar

@@ -42,14 +42,18 @@ def tile_list_sigm_biasP_kernel(
         sigs = [keep.tile([P, SUB, PACK], F32, name=f"sig{k}") for k in range(DEPTH)]
         h_bfs = [keep.tile([P, CHUNK, PACK], BF16, name=f"h_bf{k}", align_bytes=64) for k in range(PASSES)]
 
+        w_rows = keep.tile([P, 64], F32, name="w_rows", align_bytes=64)
+        nc.sync.dma_start(w_rows[:], wgt[0:P:PER_COL, :].rearrange("g (r c) -> g r c", c=64))
         offsets = keep.tile([P, J // PER_COL], U16, name="offsets")
         nc.sync.dma_start(offsets[:], offs)
 
-        raw_scales = [keep.tile([P, R], U8, name=f"raw_scales{w}") for w in range(2)]
+        raw_scales = []
         warm = keep.tile([P, 8], F32, name="warm")
 
         def load_scales(w, scales):
-            nc.vector.memset(raw_scales[w][:].bitcast(I32), 0)
+            tag = ("raw_scales0", "plane1")[w]
+            raw_scales.append(keep.tile([P, R], U8, name=f"raw_scales{w}", tag=tag, align_bytes=64))
+            (nc.vector, nc.gpsimd)[w].memset(raw_scales[w][:].bitcast(I32), 0)
             for q in range(4):
                 nc.scalar.dma_start(
                     raw_scales[w][32 * q : 32 * q + 4, :].bitcast(I32), scales[0, 4 * q : 4 * q + 4, :].bitcast(I32)
@@ -58,16 +62,12 @@ def tile_list_sigm_biasP_kernel(
         load_scales(0, wg_scales)
         nc.vector.memset(warm[:, 0:1], 0.0)
         nc.scalar.activation(warm[:, 4:5], warm[:, 0:1], ACT.Sigmoid)
-        load_scales(1, wu_scales)
 
         half = J // 2
-        weights = [keep.tile([P, half], F32, name=f"weight{i}") for i in range(2)]
+        weights = [keep.tile([P, half], F32, name=f"weight{i}", align_bytes=64) for i in range(2)]
         planes = [keep.tile([P, T], F32, name=f"plane{i}", align_bytes=64) for i in range(PACK)]
         x_planes = xT.rearrange("(p i) t -> i p t", i=PACK)
-        nc.sync.dma_start(weights[0][:], wgt[:, :half])
-        nc.sync.dma_start(planes[0][:], x_planes[0])
-        nc.sync.dma_start(weights[1][:], wgt[:, half:])
-        for i in range(1, PACK):
+        for i in range(PACK):
             nc.sync.dma_start(planes[i][:], x_planes[i])
 
         raw_words = [keep.tile([P, 2 * R], U8, name=f"raw_words{w}") for w in range(2)]
@@ -81,6 +81,19 @@ def tile_list_sigm_biasP_kernel(
                 nc.sync.dma_start(wd_raw[a][:, t, :], wd_rows[a, t])
         bias = keep.tile([P, PACK], F32, name="bias")
         nc.sync.dma_start(bias[:], b.rearrange("(p t) -> p t", t=PACK))
+
+        w_turned = keep.tile([P, 64], F32, name="w_turned", align_bytes=64)
+        for k in range(2):
+            nc.vector.transpose(w_turned[:, 32 * k : 32 * (k + 1)], w_rows[:, 32 * k : 32 * (k + 1)])
+        w_spread = [keep.tile([P, half], F32, name=f"w_spread{i}", align_bytes=64) for i in range(2)]
+        for i in range(2):
+            src = w_turned[:].rearrange("p (b h r) -> p r b h", b=2, h=2)[:, 8 * i : 8 * (i + 1)]
+            nc.vector.tensor_copy(
+                w_spread[i][:].rearrange("p (r b h s) -> p r b h s", b=2, h=2, s=PER_COL),
+                src.unsqueeze(4).to_broadcast([P, 8, 2, 2, PER_COL]),
+            )
+        for i in range(2):
+            nc.vector.transpose(weights[i][:], w_spread[i][:])
 
         low = keep.tile([P, 2, J], F32, name="low")
         high = keep.tile([P, CHUNKS + 2, CHUNK], F32, name="high")
@@ -113,11 +126,11 @@ def tile_list_sigm_biasP_kernel(
                 gather(low[:, i, j0 : j0 + half], i, j0, j0 + half)
             if i == 0:
                 deal_scales(0)
+        load_scales(1, wu_scales)
         for c in range(CHUNKS):
             weave_pair(c, 0, low[:, :, c * CHUNK : (c + 1) * CHUNK])
         for c in range(0, CHUNKS, 2):
             gather(high[:, c : c + 2, :].rearrange("p c j -> p (c j)"), 2, c * CHUNK, (c + 2) * CHUNK)
-        deal_scales(1)
 
         def last_plane(c):
             row = CHUNKS + c % 2
@@ -142,6 +155,7 @@ def tile_list_sigm_biasP_kernel(
         last_plane(1)
         quantize_x(0)
         deal_words(1)
+        deal_scales(1)
 
         wd_codes = [keep.tile([P, N], U32, name=f"wd_codes{a}", align_bytes=64) for a in range(PASSES)]
         wd_scales = [keep.tile([P, N], U8, name=f"wd_scales{a}", align_bytes=64) for a in range(PASSES)]

@@ -25,8 +25,13 @@ CHUNKS = J // CHUNK
 SUB = 128
 PER_COL = 16
 DEPTH = 3
-ON_SCALAR = (1, 2)
-WD_AT = (1, 2, 3, 4, 4, 5, 5, 6)
+SIGS = 8
+CAST_ON_SCALAR = (0,)
+ON_SCALAR = (0, 2)
+WD_AT = (0, 4)
+WD_PER_UNIT = 2
+PLANES_AT = (11, 13)
+WORD_STORES = (512, 768, 1024)
 
 
 def tile_list_sigm_biasP_kernel(
@@ -39,7 +44,7 @@ def tile_list_sigm_biasP_kernel(
         gate_banks = [psum.tile([P, PACK, SUB], F32, name=f"gate{k}") for k in range(DEPTH)]
         up_banks = [psum.tile([P, PACK, SUB], F32, name=f"up{k}") for k in range(DEPTH)]
         y_banks = [psum.tile([P, 2, CHUNK], F32, name=f"y_sum{k}") for k in range(2)]
-        sigs = [keep.tile([P, SUB, PACK], F32, name=f"sig{k}") for k in range(DEPTH)]
+        sigs = [keep.tile([P, SUB, PACK], F32, name=f"sig{k}") for k in range(SIGS)]
         h_bfs = [keep.tile([P, CHUNK, PACK], BF16, name=f"h_bf{k}", align_bytes=64) for k in range(PASSES)]
 
         w_rows = keep.tile([P, 64], F32, name="w_rows", align_bytes=64)
@@ -64,7 +69,7 @@ def tile_list_sigm_biasP_kernel(
         nc.scalar.activation(warm[:, 4:5], warm[:, 0:1], ACT.Sigmoid)
 
         half = J // 2
-        weights = [keep.tile([P, half], F32, name=f"weight{i}", align_bytes=64) for i in range(2)]
+        weight = keep.tile([P, J], F32, name="weight", align_bytes=64)
         planes = [keep.tile([P, T], F32, name=f"plane{i}", align_bytes=64) for i in range(PACK)]
         x_planes = xT.rearrange("(p i) t -> i p t", i=PACK)
         for i in range(PACK):
@@ -93,7 +98,7 @@ def tile_list_sigm_biasP_kernel(
                 src.unsqueeze(4).to_broadcast([P, 8, 2, 2, PER_COL]),
             )
         for i in range(2):
-            nc.vector.transpose(weights[i][:], w_spread[i][:])
+            nc.vector.transpose(weight[:, i * half : (i + 1) * half], w_spread[i][:])
 
         low = keep.tile([P, 2, J], F32, name="low")
         high = keep.tile([P, CHUNKS + 2, CHUNK], F32, name="high")
@@ -105,12 +110,12 @@ def tile_list_sigm_biasP_kernel(
             nc.vector.tensor_tensor(
                 out,
                 planes[i][:].indirect(offsets[:, j0 // PER_COL : j1 // PER_COL]),
-                weights[j0 // half][:, j0 % half : j0 % half + j1 - j0],
+                weight[:, j0:j1],
                 MULT,
             )
 
-        def weave_pair(c, pair, src):
-            nc.scalar.copy(x_bf[c][:, :, 2 * pair : 2 * pair + 2], src.rearrange("p t j -> p j t"))
+        def weave_pair(c, pair, src, cols):
+            nc.scalar.copy(x_bf[c][:, cols, 2 * pair : 2 * pair + 2], src[:, :, cols].rearrange("p t j -> p j t"))
 
         w_scales = []
 
@@ -121,25 +126,25 @@ def tile_list_sigm_biasP_kernel(
                 raw_scales[w][:].bitcast(I32).rearrange("p (g q t) -> p g q t", t=PACK, q=32),
             )
 
-        for i in range(2):
-            for j0 in range(0, J, half):
-                gather(low[:, i, j0 : j0 + half], i, j0, j0 + half)
-            if i == 0:
-                deal_scales(0)
+        gather(low[:, 0, :], 0, 0, J)
+        deal_scales(0)
+        for j0 in range(0, J, half):
+            gather(low[:, 1, j0 : j0 + half], 1, j0, j0 + half)
         load_scales(1, wu_scales)
         for c in range(CHUNKS):
-            weave_pair(c, 0, low[:, :, c * CHUNK : (c + 1) * CHUNK])
-        for c in range(0, CHUNKS, 2):
-            gather(high[:, c : c + 2, :].rearrange("p c j -> p (c j)"), 2, c * CHUNK, (c + 2) * CHUNK)
+            weave_pair(c, 0, low[:, :, c * CHUNK : (c + 1) * CHUNK], slice(0, CHUNK))
+        gather(high[:, :CHUNKS, :].rearrange("p c j -> p (c j)"), 2, 0, J)
 
-        def last_plane(c):
+        def last_plane(c, cols):
             row = CHUNKS + c % 2
-            gather(high[:, row, :], 3, c * CHUNK, (c + 1) * CHUNK)
-            weave_pair(c, 1, high[:, c : row + 1 : row - c, :])
+            gather(high[:, row, cols], 3, c * CHUNK + cols.start, c * CHUNK + cols.stop)
+            weave_pair(c, 1, high[:, c : row + 1 : row - c, :], cols)
 
-        def quantize_x(c):
+        def quantize_x(c, cols):
             nc.vector.quantize_mx(
-                out=x_codes[c][:].bitcast(FP8X4), scales=x_scales[c][:], in_=x_bf[c][:].rearrange("p j t -> p (j t)")
+                out=x_codes[c][:, cols].bitcast(FP8X4),
+                scales=x_scales[c][:, cols],
+                in_=x_bf[c][:, cols, :].rearrange("p j t -> p (j t)"),
             )
 
         w_words = [keep.tile([P, 2 * R], U8, name=f"w_words{w}", align_bytes=64) for w in range(2)]
@@ -150,12 +155,16 @@ def tile_list_sigm_biasP_kernel(
                 raw_words[w][:].bitcast(I32).rearrange("p (a q t h) -> p a q t h", t=PACK, q=32, h=2),
             )
 
-        last_plane(0)
+        whole = slice(0, CHUNK)
+        subs = [slice(0, SUB), slice(SUB, CHUNK)]
+        last_plane(0, subs[0])
+        last_plane(0, subs[1])
         deal_words(0)
-        last_plane(1)
-        quantize_x(0)
+        quantize_x(0, subs[0])
         deal_words(1)
         deal_scales(1)
+        last_plane(1, whole)
+        quantize_x(0, subs[1])
 
         wd_codes = [keep.tile([P, N], U32, name=f"wd_codes{a}", align_bytes=64) for a in range(PASSES)]
         wd_scales = [keep.tile([P, N], U8, name=f"wd_scales{a}", align_bytes=64) for a in range(PASSES)]
@@ -189,7 +198,7 @@ def tile_list_sigm_biasP_kernel(
                         start=True,
                         stop=True,
                     )
-            sig = sigs[unit % DEPTH][:]
+            sig = sigs[unit % SIGS][:]
             nc.scalar.activation(sig, sums[0][:].rearrange("p t j -> p j t"), ACT.Sigmoid)
             nc.vector.tensor_tensor(h_bfs[a][:, cols, :], sums[1][:].rearrange("p t j -> p j t"), sig, MULT)
 
@@ -202,6 +211,7 @@ def tile_list_sigm_biasP_kernel(
             )
 
         y_scales = keep.tile([P, J], U8, name="y_scales", align_bytes=64)
+        y_codes = keep.tile([P, J], U32, name="y_codes", align_bytes=64)
         y_rows = out_0.rearrange("(p u) j -> p u j", u=PACK)
         y_words = out_1[0].rearrange("p j i -> p (j i)").bitcast(I32)
 
@@ -233,29 +243,33 @@ def tile_list_sigm_biasP_kernel(
         def planes_of(j0, width, y):
             cols = slice(j0, j0 + width)
             y_bf = keep.tile([P, width * PACK], BF16, name=f"y_bf{j0}", align_bytes=64)
-            nc.vector.tensor_copy(
+            (nc.scalar.copy if j0 in CAST_ON_SCALAR else nc.vector.tensor_copy)(
                 y_bf[:].rearrange("p (g i u) -> p g u i", i=4, u=PACK),
                 y[:].rearrange("p u (g i) -> p g u i", i=4),
             )
-            y_codes = keep.tile([P, width], U32, name=f"y_codes{j0}", align_bytes=64)
-            nc.vector.quantize_mx(out=y_codes[:].bitcast(FP8X4), scales=y_scales[:, cols], in_=y_bf[:])
-            nc.sync.dma_start(y_words[:, cols], y_codes[:].bitcast(I32))
+            nc.vector.quantize_mx(out=y_codes[:, cols].bitcast(FP8X4), scales=y_scales[:, cols], in_=y_bf[:])
+            if j0 + width in WORD_STORES:
+                done = slice(max(e for e in (0,) + WORD_STORES if e < j0 + width), j0 + width)
+                nc.sync.dma_start(y_words[:, done], y_codes[:, done].bitcast(I32))
 
         last = CHUNKS - 1
-        units = [(c, a, s) for c in range(last) for a in range(PASSES) for s in range(2)]
-        units = units + [(last, a, s) for s in range(2) for a in range(PASSES)]
+        by_sub = [(a, s) for s in range(2) for a in range(PASSES)]
+        by_pass = [(a, s) for a in range(PASSES) for s in range(2)]
+        units = [(c, a, s) for c in range(CHUNKS) for a, s in (by_sub if c in (0, last) else by_pass)]
+        wd_done = WD_AT[-1] + (PACK - 1) // WD_PER_UNIT
         ys = {}
         for unit, (c, a, s) in enumerate(units):
             hidden(unit, c, a, s)
             if unit < 2:
                 if unit == 0:
-                    quantize_x(1)
-                last_plane(2 + unit)
+                    quantize_x(1, whole)
+                last_plane(2 + unit, whole)
             elif unit < 4:
-                quantize_x(unit)
-            for k, at in enumerate(WD_AT):
-                if at == unit:
-                    weave_wd(k // PACK, k % PACK)
+                quantize_x(unit, whole)
+            for wa in range(PASSES):
+                for k in range(PACK):
+                    if WD_AT[wa] + k // WD_PER_UNIT == unit:
+                        weave_wd(wa, k)
             if unit >= 1:
                 pc, pa, ps = units[unit - 1]
                 if pc == last:
@@ -263,10 +277,10 @@ def tile_list_sigm_biasP_kernel(
                 elif ps == 1:
                     quantize_h(pa, pc * CHUNK, CHUNK)
             for d in range(last):
-                ready = max(4 * d + 4, max(WD_AT))
-                if unit == ready:
+                if unit == max(4 * d + 4, wd_done):
                     ys[d] = down(d * CHUNK, CHUNK, y_banks, False)
-                if unit == ready + 2:
+            for d, at in enumerate(PLANES_AT):
+                if unit == at:
                     planes_of(d * CHUNK, CHUNK, ys[d])
             if unit == len(units) - 2:
                 tail = [gate_banks[(unit - 1) % DEPTH][:, 0:2, :], gate_banks[unit % DEPTH][:, 0:2, :]]
@@ -274,7 +288,9 @@ def tile_list_sigm_biasP_kernel(
         unit = len(units) - 1
         quantize_h(PASSES - 1, J - SUB, SUB)
         tail = [gate_banks[unit % DEPTH][:, 0:2, :], up_banks[(unit - 2) % DEPTH][:, 0:2, :]]
-        y_end = down(J - SUB, SUB, tail, True)
+        y_end = down(J - SUB, SUB, tail, False)
+        for d in range(len(PLANES_AT), last):
+            planes_of(d * CHUNK, CHUNK, ys[d])
         planes_of(last * CHUNK, SUB, ys[last])
         planes_of(J - SUB, SUB, y_end)
 

@@ -27,10 +27,9 @@ PER_COL = 16
 DEPTH = 3
 SIGS = 8
 CAST_ON_SCALAR = (0,)
-ON_SCALAR = (0, 2)
 WD_AT = (0, 4)
-WD_PER_UNIT = 2
-PLANES_AT = (11, 13)
+DOWN_AT = (9, 12, 14)
+PLANES_AT = (14,)
 WORD_STORES = (512, 768, 1024)
 
 
@@ -48,7 +47,7 @@ def tile_list_sigm_biasP_kernel(
         h_bfs = [keep.tile([P, CHUNK, PACK], BF16, name=f"h_bf{k}", align_bytes=64) for k in range(PASSES)]
 
         w_rows = keep.tile([P, 64], F32, name="w_rows", align_bytes=64)
-        nc.sync.dma_start(w_rows[:], wgt[0:P:PER_COL, :].rearrange("g (r c) -> g r c", c=64))
+        nc.scalar.dma_start(w_rows[:], wgt[0:P:PER_COL, :].rearrange("g (r c) -> g r c", c=64))
         offsets = keep.tile([P, J // PER_COL], U16, name="offsets")
         nc.sync.dma_start(offsets[:], offs)
 
@@ -120,14 +119,13 @@ def tile_list_sigm_biasP_kernel(
         w_scales = []
 
         def deal_scales(w):
-            w_scales.append(keep.tile([P, R], U8, name=f"w_scales{w}", tag=f"plane{2 * w}", align_bytes=64))
+            w_scales.append(keep.tile([P, R], U8, name=f"w_scales{w}", tag=("plane2", "w_scales1")[w], align_bytes=64))
             nc.vector.tensor_copy(
                 w_scales[w][:].bitcast(I32).rearrange("p (g t q) -> p g q t", t=PACK, q=32),
                 raw_scales[w][:].bitcast(I32).rearrange("p (g q t) -> p g q t", t=PACK, q=32),
             )
 
         gather(low[:, 0, :], 0, 0, J)
-        deal_scales(0)
         for j0 in range(0, J, half):
             gather(low[:, 1, j0 : j0 + half], 1, j0, j0 + half)
         load_scales(1, wu_scales)
@@ -160,6 +158,7 @@ def tile_list_sigm_biasP_kernel(
         last_plane(0, subs[0])
         last_plane(0, subs[1])
         deal_words(0)
+        deal_scales(0)
         quantize_x(0, subs[0])
         deal_words(1)
         deal_scales(1)
@@ -170,14 +169,11 @@ def tile_list_sigm_biasP_kernel(
         wd_scales = [keep.tile([P, N], U8, name=f"wd_scales{a}", align_bytes=64) for a in range(PASSES)]
         wd_bf = [keep.tile([P, N * PACK], BF16, name=f"wd_bf{a}", align_bytes=64) for a in range(PASSES)]
 
-        def weave_wd(a, k):
-            dst = wd_bf[a][:].rearrange("p (u m t) -> p m t u", u=PACK, t=PACK)[:, 32 * k : 32 * (k + 1)]
-            src = wd_raw[a][:, :, P * k : P * (k + 1)].rearrange("p t (m u) -> p m t u", u=PACK)
-            if k >= PACK - ON_SCALAR[a]:
-                nc.scalar.copy(dst, src)
-            else:
-                nc.vector.tensor_copy(dst, src)
-            if k == PACK - 1:
+        def weave_wd(a, k, copy):
+            dst = wd_bf[a][:].rearrange("p (u m t) -> p m t u", u=PACK, t=PACK)[:, 64 * k : 64 * (k + 1)]
+            src = wd_raw[a][:, :, 2 * P * k : 2 * P * (k + 1)].rearrange("p t (m u) -> p m t u", u=PACK)
+            copy(dst, src)
+            if k == 1:
                 nc.vector.quantize_mx(out=wd_codes[a][:].bitcast(FP8X4), scales=wd_scales[a][:], in_=wd_bf[a][:])
 
         h_codes = [keep.tile([P, J], U32, name=f"h_codes{a}", align_bytes=64) for a in range(PASSES)]
@@ -256,7 +252,6 @@ def tile_list_sigm_biasP_kernel(
         by_sub = [(a, s) for s in range(2) for a in range(PASSES)]
         by_pass = [(a, s) for a in range(PASSES) for s in range(2)]
         units = [(c, a, s) for c in range(CHUNKS) for a, s in (by_sub if c in (0, last) else by_pass)]
-        wd_done = WD_AT[-1] + (PACK - 1) // WD_PER_UNIT
         ys = {}
         for unit, (c, a, s) in enumerate(units):
             hidden(unit, c, a, s)
@@ -267,9 +262,9 @@ def tile_list_sigm_biasP_kernel(
             elif unit < 4:
                 quantize_x(unit, whole)
             for wa in range(PASSES):
-                for k in range(PACK):
-                    if WD_AT[wa] + k // WD_PER_UNIT == unit:
-                        weave_wd(wa, k)
+                for k in range(2):
+                    if WD_AT[wa] + k == unit:
+                        weave_wd(wa, k, nc.scalar.copy if (wa, k) == (1, 1) else nc.vector.tensor_copy)
             if unit >= 1:
                 pc, pa, ps = units[unit - 1]
                 if pc == last:
@@ -277,7 +272,7 @@ def tile_list_sigm_biasP_kernel(
                 elif ps == 1:
                     quantize_h(pa, pc * CHUNK, CHUNK)
             for d in range(last):
-                if unit == max(4 * d + 4, wd_done):
+                if unit == DOWN_AT[d]:
                     ys[d] = down(d * CHUNK, CHUNK, y_banks, False)
             for d, at in enumerate(PLANES_AT):
                 if unit == at:

@@ -25,8 +25,8 @@ CHUNKS = J // CHUNK
 SUB = 128
 PER_COL = 16
 DEPTH = 3
-SIGS = 8
-CAST_ON_SCALAR = (0,)
+SIGS = 4
+CAST_ON_SCALAR = ()
 WD_AT = (0, 4)
 DOWN_AT = (9, 12, 14)
 PLANES_AT = (14,)
@@ -40,10 +40,10 @@ def tile_list_sigm_biasP_kernel(
     with ExitStack() as ctx:
         keep = ctx.enter_context(tc.tile_pool(name="keep", bufs=1))
         psum = ctx.enter_context(tc.psum_pool(name="psum", bufs=1))
-        gate_banks = [psum.tile([P, PACK, SUB], F32, name=f"gate{k}") for k in range(DEPTH)]
+        gate_banks = [psum.tile([P, 2, CHUNK], F32, name=f"gate{k}") for k in range(DEPTH)]
         up_banks = [psum.tile([P, PACK, SUB], F32, name=f"up{k}") for k in range(DEPTH)]
         y_banks = [psum.tile([P, 2, CHUNK], F32, name=f"y_sum{k}") for k in range(2)]
-        sigs = [keep.tile([P, SUB, PACK], F32, name=f"sig{k}") for k in range(SIGS)]
+        sigs = [keep.tile([P, 2, CHUNK, 2], F32, name=f"sig{k}") for k in range(SIGS)]
         h_bfs = [keep.tile([P, CHUNK, PACK], BF16, name=f"h_bf{k}", align_bytes=64) for k in range(PASSES)]
 
         w_rows = keep.tile([P, 64], F32, name="w_rows", align_bytes=64)
@@ -179,24 +179,41 @@ def tile_list_sigm_biasP_kernel(
         h_codes = [keep.tile([P, J], U32, name=f"h_codes{a}", align_bytes=64) for a in range(PASSES)]
         h_scales = [keep.tile([P, J], U8, name=f"h_scales{a}", align_bytes=64) for a in range(PASSES)]
 
+        def first_stage(out, w, a, t, c, cols):
+            r0 = (a * PACK + t) * P
+            nc.tensor.matmul_mx(
+                out=out,
+                lhsT=w_words[w][:, 2 * r0 : 2 * (r0 + P)].bitcast(FP4X4),
+                lhsT_scale=w_scales[w][:, r0 : r0 + P],
+                rhs=x_codes[c][:, cols].bitcast(FP8X4),
+                rhs_scale=x_scales[c][:, cols],
+                start=True,
+                stop=True,
+            )
+
         def hidden(unit, c, a, s):
             cols = slice(s * SUB, (s + 1) * SUB)
-            sums = (gate_banks[unit % DEPTH], up_banks[unit % DEPTH])
-            for w in range(2):
+            sig = sigs[(PASSES * c + a) % SIGS]
+            if c == 0:
+                bank = gate_banks[unit % DEPTH][:].rearrange("p v (h j) -> p (v h) j", h=2)
                 for t in range(PACK):
-                    r0 = (a * PACK + t) * P
-                    nc.tensor.matmul_mx(
-                        out=sums[w][:, t, :],
-                        lhsT=w_words[w][:, 2 * r0 : 2 * (r0 + P)].bitcast(FP4X4),
-                        lhsT_scale=w_scales[w][:, r0 : r0 + P],
-                        rhs=x_codes[c][:, cols].bitcast(FP8X4),
-                        rhs_scale=x_scales[c][:, cols],
-                        start=True,
-                        stop=True,
-                    )
-            sig = sigs[unit % SIGS][:]
-            nc.scalar.activation(sig, sums[0][:].rearrange("p t j -> p j t"), ACT.Sigmoid)
-            nc.vector.tensor_tensor(h_bfs[a][:, cols, :], sums[1][:].rearrange("p t j -> p j t"), sig, MULT)
+                    first_stage(bank[:, t, :], 0, a, t, c, cols)
+                nc.scalar.activation(sig[:, :, cols, :], bank.rearrange("p (k v) j -> p k j v", v=2), ACT.Sigmoid)
+            elif s == 0:
+                for k in range(2):
+                    bank = gate_banks[(2 * (PASSES * c + a) + k) % DEPTH]
+                    for v in range(2):
+                        first_stage(bank[:, v, :], 0, a, 2 * k + v, c, whole)
+                    nc.scalar.activation(sig[:, k], bank[:].rearrange("p v j -> p j v"), ACT.Sigmoid)
+            bank = up_banks[unit % DEPTH]
+            for t in range(PACK):
+                first_stage(bank[:, t, :], 1, a, t, c, cols)
+            nc.vector.tensor_tensor(
+                h_bfs[a][:, cols, :].rearrange("p j (k v) -> p j k v", v=2),
+                bank[:].rearrange("p (k v) j -> p j k v", v=2),
+                sig[:, :, cols, :].rearrange("p k j v -> p j k v"),
+                MULT,
+            )
 
         def quantize_h(a, j0, width):
             s0 = j0 % CHUNK
@@ -278,11 +295,11 @@ def tile_list_sigm_biasP_kernel(
                 if unit == at:
                     planes_of(d * CHUNK, CHUNK, ys[d])
             if unit == len(units) - 2:
-                tail = [gate_banks[(unit - 1) % DEPTH][:, 0:2, :], gate_banks[unit % DEPTH][:, 0:2, :]]
+                tail = [gate_banks[(unit - 1) % DEPTH][:, :, :SUB], gate_banks[unit % DEPTH][:, :, :SUB]]
                 ys[last] = down(last * CHUNK, SUB, tail, False)
         unit = len(units) - 1
         quantize_h(PASSES - 1, J - SUB, SUB)
-        tail = [gate_banks[unit % DEPTH][:, 0:2, :], up_banks[(unit - 2) % DEPTH][:, 0:2, :]]
+        tail = [gate_banks[unit % DEPTH][:, :, :SUB], up_banks[(unit - 2) % DEPTH][:, 0:2, :]]
         y_end = down(J - SUB, SUB, tail, False)
         for d in range(len(PLANES_AT), last):
             planes_of(d * CHUNK, CHUNK, ys[d])

@@ -25,11 +25,12 @@ CHUNKS = J // CHUNK
 SUB = 128
 PER_COL = 16
 DEPTH = 3
-SIGS = 4
-CAST_ON_SCALAR = ()
-WD_AT = (0, 4)
-DOWN_AT = (9, 12, 14)
-PLANES_AT = (14,)
+PIECE = CHUNK * PACK
+LEAD = 5
+Y_ON_SCALAR = ()
+G_ROWS = (80, 96)
+S_AT = (4, 5)
+DOWN_AT = (8, 12, 15)
 WORD_STORES = (512, 768, 1024)
 
 
@@ -43,8 +44,8 @@ def tile_list_sigm_biasP_kernel(
         gate_banks = [psum.tile([P, 2, CHUNK], F32, name=f"gate{k}") for k in range(DEPTH)]
         up_banks = [psum.tile([P, PACK, SUB], F32, name=f"up{k}") for k in range(DEPTH)]
         y_banks = [psum.tile([P, 2, CHUNK], F32, name=f"y_sum{k}") for k in range(2)]
-        sigs = [keep.tile([P, 2, CHUNK, 2], F32, name=f"sig{k}") for k in range(SIGS)]
-        h_bfs = [keep.tile([P, CHUNK, PACK], BF16, name=f"h_bf{k}", align_bytes=64) for k in range(PASSES)]
+        sigs = [keep.tile([P, 2, CHUNK, 2], F32, name=f"sig{k}", align_bytes=64) for k in range(CHUNKS * PASSES)]
+        stage = [keep.tile([P, PASSES * PIECE], BF16, name=f"stage{k}", align_bytes=64) for k in range(2)]
 
         w_rows = keep.tile([P, 64], F32, name="w_rows", align_bytes=64)
         nc.scalar.dma_start(w_rows[:], wgt[0:P:PER_COL, :].rearrange("g (r c) -> g r c", c=64))
@@ -71,12 +72,12 @@ def tile_list_sigm_biasP_kernel(
         weight = keep.tile([P, J], F32, name="weight", align_bytes=64)
         planes = [keep.tile([P, T], F32, name=f"plane{i}", align_bytes=64) for i in range(PACK)]
         x_planes = xT.rearrange("(p i) t -> i p t", i=PACK)
-        for i in range(PACK):
-            nc.sync.dma_start(planes[i][:], x_planes[i])
-
         raw_words = [keep.tile([P, 2 * R], U8, name=f"raw_words{w}") for w in range(2)]
-        for w, words in enumerate((wg_words, wu_words)):
-            nc.sync.dma_start(raw_words[w][:].bitcast(I32), words[0].bitcast(I32))
+        for i in range(PACK - 1):
+            nc.sync.dma_start(planes[i][:], x_planes[i])
+        nc.sync.dma_start(raw_words[0][:].bitcast(I32), wg_words[0].bitcast(I32))
+        nc.sync.dma_start(planes[PACK - 1][:], x_planes[PACK - 1])
+        nc.sync.dma_start(raw_words[1][:].bitcast(I32), wu_words[0].bitcast(I32))
 
         wd_raw = [keep.tile([P, PACK, N], F32, name=f"wd_raw{a}") for a in range(PASSES)]
         wd_rows = wd.rearrange("(a q t e) n -> a t q e n", a=PASSES, t=PACK, e=4)
@@ -100,10 +101,19 @@ def tile_list_sigm_biasP_kernel(
             nc.vector.transpose(weight[:, i * half : (i + 1) * half], w_spread[i][:])
 
         low = keep.tile([P, 2, J], F32, name="low")
-        high = keep.tile([P, CHUNKS + 2, CHUNK], F32, name="high")
-        x_bf = [keep.tile([P, CHUNK, PACK], BF16, name=f"x_bf{c}", align_bytes=64) for c in range(CHUNKS)]
-        x_codes = [keep.tile([P, CHUNK], U32, name=f"x_codes{c}", align_bytes=64) for c in range(CHUNKS)]
-        x_scales = [keep.tile([P, CHUNK], U8, name=f"x_scales{c}", align_bytes=64) for c in range(CHUNKS)]
+        high_flat = keep.tile([P, 2 * J], F32, name="high", align_bytes=64)
+        high = high_flat[:].rearrange("p (t j) -> p t j", t=2)
+        x_head = keep.tile([P, PIECE // 2], BF16, name="x_head", align_bytes=64)
+        x_second = keep.tile([P, PIECE], BF16, name="x_second", align_bytes=64)
+        x_late = keep.tile([P, 2 * PIECE], BF16, name="x_late", align_bytes=64)
+        x_parts = {
+            (0, SUB): x_head[:],
+            (SUB, CHUNK): high_flat[:, 2 * J - CHUNK :].bitcast(BF16),
+            (CHUNK, 2 * CHUNK): x_second[:],
+            (half, J): x_late[:],
+        }
+        x_codes = [keep.tile([P, CHUNK], U32, name=f"x_codes{c}", align_bytes=64)[:] for c in range(2)]
+        x_scales = [keep.tile([P, CHUNK], U8, name=f"x_scales{c}", align_bytes=64)[:] for c in range(2)]
 
         def gather(out, i, j0, j1):
             nc.vector.tensor_tensor(
@@ -113,71 +123,79 @@ def tile_list_sigm_biasP_kernel(
                 MULT,
             )
 
-        def weave_pair(c, pair, src, cols):
-            nc.scalar.copy(x_bf[c][:, cols, 2 * pair : 2 * pair + 2], src[:, :, cols].rearrange("p t j -> p j t"))
+        def weave_pair(pair, j0, j1, copy=nc.scalar.copy):
+            dst = x_parts[j0, j1].rearrange("p (j t) -> p j t", t=PACK)[:, :, 2 * pair : 2 * pair + 2]
+            copy(dst, (low, high)[pair][:, :, j0:j1].rearrange("p t j -> p j t"))
 
+        w_words = []
         w_scales = []
 
-        def deal_scales(w):
-            w_scales.append(keep.tile([P, R], U8, name=f"w_scales{w}", tag=("plane2", "w_scales1")[w], align_bytes=64))
+        def deal(w):
+            dealt = keep.tile([P, 3 * R], U8, name=f"dealt{w}", tag=("plane2", "x_head")[w], align_bytes=64)
+            w_words.append(dealt[:, : 2 * R])
+            w_scales.append(dealt[:, 2 * R :])
             nc.vector.tensor_copy(
-                w_scales[w][:].bitcast(I32).rearrange("p (g t q) -> p g q t", t=PACK, q=32),
+                w_words[w].bitcast(I32).rearrange("p (a t q h) -> p a q t h", t=PACK, q=32, h=2),
+                raw_words[w][:].bitcast(I32).rearrange("p (a q t h) -> p a q t h", t=PACK, q=32, h=2),
+            )
+            nc.vector.tensor_copy(
+                w_scales[w].bitcast(I32).rearrange("p (g t q) -> p g q t", t=PACK, q=32),
                 raw_scales[w][:].bitcast(I32).rearrange("p (g q t) -> p g q t", t=PACK, q=32),
             )
 
+        whole = slice(0, CHUNK)
         gather(low[:, 0, :], 0, 0, J)
         for j0 in range(0, J, half):
             gather(low[:, 1, j0 : j0 + half], 1, j0, j0 + half)
         load_scales(1, wu_scales)
-        for c in range(CHUNKS):
-            weave_pair(c, 0, low[:, :, c * CHUNK : (c + 1) * CHUNK], slice(0, CHUNK))
-        gather(high[:, :CHUNKS, :].rearrange("p c j -> p (c j)"), 2, 0, J)
+        for j0, j1 in x_parts:
+            weave_pair(0, j0, j1)
+        gather(high[:, 0, :], 2, 0, J)
+        deal(0)
 
-        def last_plane(c, cols):
-            row = CHUNKS + c % 2
-            gather(high[:, row, cols], 3, c * CHUNK + cols.start, c * CHUNK + cols.stop)
-            weave_pair(c, 1, high[:, c : row + 1 : row - c, :], cols)
+        def last_plane(j0, j1):
+            gather(high[:, 1, j0:j1], 3, j0, j1)
 
-        def quantize_x(c, cols):
-            nc.vector.quantize_mx(
-                out=x_codes[c][:, cols].bitcast(FP8X4),
-                scales=x_scales[c][:, cols],
-                in_=x_bf[c][:, cols, :].rearrange("p j t -> p (j t)"),
+        def quantize(codes, scales, values):
+            nc.vector.quantize_mx(out=codes.bitcast(FP8X4), scales=scales, in_=values)
+
+        def quantize_x(j0, j1):
+            c, cols = j0 // CHUNK, slice(j0 % CHUNK, j0 % CHUNK + j1 - j0)
+            quantize(x_codes[c][:, cols], x_scales[c][:, cols], x_parts[j0, j1])
+
+        early = list(x_parts)[:3]
+        for j0, j1 in early:
+            last_plane(j0, j1)
+            weave_pair(1, j0, j1)
+        quantize_x(*early[0])
+        quantize_x(*early[1])
+        deal(1)
+        last_plane(half, J)
+        quantize_x(*early[2])
+        weave_pair(1, half, J, nc.vector.tensor_copy)
+
+        wd_codes = {}
+        wd_scales = {}
+
+        def cast_on_gpsimd(dst, src):
+            nc.gpsimd.tensor_scalar(dst, src, 1.0, 0.0, MULT, ADD)
+
+        def weave_wd(a, rows, dst, cast, walk):
+            cast(
+                dst.rearrange("p (u m t) -> p " + walk, u=PACK, t=PACK)[:, rows],
+                wd_raw[a][:].rearrange("p t (m u) -> p " + walk, u=PACK)[:, rows],
             )
 
-        w_words = [keep.tile([P, 2 * R], U8, name=f"w_words{w}", align_bytes=64) for w in range(2)]
+        def mx_tile(width, name, tag):
+            both = keep.tile([P, 5 * width], U8, name=name, tag=tag, align_bytes=64)
+            return both[:, : 4 * width].bitcast(U32), both[:, 4 * width :]
 
-        def deal_words(w):
-            nc.vector.tensor_copy(
-                w_words[w][:].bitcast(I32).rearrange("p (a t q h) -> p a q t h", t=PACK, q=32, h=2),
-                raw_words[w][:].bitcast(I32).rearrange("p (a q t h) -> p a q t h", t=PACK, q=32, h=2),
-            )
+        def quantize_wd(a, src):
+            wd_codes[a], wd_scales[a] = mx_tile(N, f"wd_mx{a}", f"wd_mx{a}")
+            quantize(wd_codes[a], wd_scales[a], src)
 
-        whole = slice(0, CHUNK)
-        subs = [slice(0, SUB), slice(SUB, CHUNK)]
-        last_plane(0, subs[0])
-        last_plane(0, subs[1])
-        deal_words(0)
-        deal_scales(0)
-        quantize_x(0, subs[0])
-        deal_words(1)
-        deal_scales(1)
-        last_plane(1, whole)
-        quantize_x(0, subs[1])
-
-        wd_codes = [keep.tile([P, N], U32, name=f"wd_codes{a}", align_bytes=64) for a in range(PASSES)]
-        wd_scales = [keep.tile([P, N], U8, name=f"wd_scales{a}", align_bytes=64) for a in range(PASSES)]
-        wd_bf = [keep.tile([P, N * PACK], BF16, name=f"wd_bf{a}", align_bytes=64) for a in range(PASSES)]
-
-        def weave_wd(a, k, copy):
-            dst = wd_bf[a][:].rearrange("p (u m t) -> p m t u", u=PACK, t=PACK)[:, 64 * k : 64 * (k + 1)]
-            src = wd_raw[a][:, :, 2 * P * k : 2 * P * (k + 1)].rearrange("p t (m u) -> p m t u", u=PACK)
-            copy(dst, src)
-            if k == 1:
-                nc.vector.quantize_mx(out=wd_codes[a][:].bitcast(FP8X4), scales=wd_scales[a][:], in_=wd_bf[a][:])
-
-        h_codes = [keep.tile([P, J], U32, name=f"h_codes{a}", align_bytes=64) for a in range(PASSES)]
-        h_scales = [keep.tile([P, J], U8, name=f"h_scales{a}", align_bytes=64) for a in range(PASSES)]
+        h_codes = [keep.tile([P, PASSES * CHUNK], U32, name=f"h_codes{c}", align_bytes=64) for c in range(CHUNKS)]
+        h_scales = [keep.tile([P, PASSES * CHUNK], U8, name=f"h_scales{c}", align_bytes=64) for c in range(CHUNKS)]
 
         def first_stage(out, w, a, t, c, cols):
             r0 = (a * PACK + t) * P
@@ -191,120 +209,140 @@ def tile_list_sigm_biasP_kernel(
                 stop=True,
             )
 
+        last = CHUNKS - 1
+
+        def h_column(c, a, s):
+            return (s * PASSES + a) * SUB if c == last else a * CHUNK + s * SUB
+
+        def gate(step):
+            bank = gate_banks[step % DEPTH]
+            if step < PACK:
+                c, a, s = units[step]
+                cols = slice(s * SUB, (s + 1) * SUB)
+                quarters = bank[:].rearrange("p v (h j) -> p (v h) j", h=2)
+                for t in range(PACK):
+                    first_stage(quarters[:, t, :], 0, a, t, c, cols)
+                nc.scalar.activation(
+                    sigs[a][:, :, cols, :], quarters.rearrange("p (k v) j -> p k j v", v=2), ACT.Sigmoid
+                )
+            else:
+                g, k = divmod(step, 2)
+                for v in range(2):
+                    first_stage(bank[:, v, :], 0, g % PASSES, 2 * k + v, g // PASSES, whole)
+                nc.scalar.activation(sigs[g][:, k], bank[:].rearrange("p v j -> p j v"), ACT.Sigmoid)
+
         def hidden(unit, c, a, s):
             cols = slice(s * SUB, (s + 1) * SUB)
-            sig = sigs[(PASSES * c + a) % SIGS]
-            if c == 0:
-                bank = gate_banks[unit % DEPTH][:].rearrange("p v (h j) -> p (v h) j", h=2)
-                for t in range(PACK):
-                    first_stage(bank[:, t, :], 0, a, t, c, cols)
-                nc.scalar.activation(sig[:, :, cols, :], bank.rearrange("p (k v) j -> p k j v", v=2), ACT.Sigmoid)
-            elif s == 0:
-                for k in range(2):
-                    bank = gate_banks[(2 * (PASSES * c + a) + k) % DEPTH]
-                    for v in range(2):
-                        first_stage(bank[:, v, :], 0, a, 2 * k + v, c, whole)
-                    nc.scalar.activation(sig[:, k], bank[:].rearrange("p v j -> p j v"), ACT.Sigmoid)
+            sig = sigs[PASSES * c + a]
             bank = up_banks[unit % DEPTH]
             for t in range(PACK):
                 first_stage(bank[:, t, :], 1, a, t, c, cols)
+            h0 = h_column(c, a, s) * PACK
             nc.vector.tensor_tensor(
-                h_bfs[a][:, cols, :].rearrange("p j (k v) -> p j k v", v=2),
+                stage[c % 2][:, h0 : h0 + SUB * PACK].rearrange("p (j k v) -> p j k v", k=2, v=2),
                 bank[:].rearrange("p (k v) j -> p j k v", v=2),
                 sig[:, :, cols, :].rearrange("p k j v -> p j k v"),
                 MULT,
             )
 
-        def quantize_h(a, j0, width):
-            s0 = j0 % CHUNK
-            nc.vector.quantize_mx(
-                out=h_codes[a][:, j0 : j0 + width].bitcast(FP8X4),
-                scales=h_scales[a][:, j0 : j0 + width],
-                in_=h_bfs[a][:, s0 : s0 + width, :].rearrange("p j t -> p (j t)"),
-            )
+        def quantize_h(c, c0, c1):
+            quantize(h_codes[c][:, c0:c1], h_scales[c][:, c0:c1], stage[c % 2][:, c0 * PACK : c1 * PACK])
 
         y_scales = keep.tile([P, J], U8, name="y_scales", align_bytes=64)
         y_codes = keep.tile([P, J], U32, name="y_codes", align_bytes=64)
         y_rows = out_0.rearrange("(p u) j -> p u j", u=PACK)
         y_words = out_1[0].rearrange("p j i -> p (j i)").bitcast(I32)
 
-        def down(j0, width, banks, share):
-            cols = slice(j0, j0 + width)
+        def down(j0, width, banks):
+            c, s = divmod(j0 // SUB, 2)
             y = keep.tile([P, PACK, width], F32, name=f"y{j0}")
             for k, bank in enumerate(banks):
                 for a in range(PASSES):
+                    cols = slice(h_column(c, a, s), h_column(c, a, s) + width)
                     for v in range(2):
-                        u = 2 * k + v
                         nc.tensor.matmul_mx(
                             out=bank[:, v, :],
-                            lhsT=wd_codes[a][:, u * P : (u + 1) * P].bitcast(FP8X4),
-                            lhsT_scale=wd_scales[a][:, u * P : (u + 1) * P],
-                            rhs=h_codes[a][:, cols].bitcast(FP8X4),
-                            rhs_scale=h_scales[a][:, cols],
+                            lhsT=wd_codes[a][:, (2 * k + v) * P : (2 * k + v + 1) * P].bitcast(FP8X4),
+                            lhsT_scale=wd_scales[a][:, (2 * k + v) * P : (2 * k + v + 1) * P],
+                            rhs=h_codes[c][:, cols].bitcast(FP8X4),
+                            rhs_scale=h_scales[c][:, cols],
                             start=(a == 0 and v == 0),
                             stop=(a == PASSES - 1 and v == 1),
                         )
                 for v in range(2):
                     u = 2 * k + v
-                    if share and k == 1:
-                        nc.vector.tensor_scalar(y[:, u, :], bank[:, v, :], bias[:, u : u + 1], None, ADD)
-                    else:
-                        nc.scalar.activation(y[:, u, :], bank[:, v, :], ACT.Identity, bias=bias[:, u : u + 1])
-            nc.sync.dma_start(y_rows[:, :, cols], y[:])
+                    nc.scalar.activation(y[:, u, :], bank[:, v, :], ACT.Identity, bias=bias[:, u : u + 1])
+            nc.sync.dma_start(y_rows[:, :, j0 : j0 + width], y[:])
             return y
 
-        def planes_of(j0, width, y):
-            cols = slice(j0, j0 + width)
-            y_bf = keep.tile([P, width * PACK], BF16, name=f"y_bf{j0}", align_bytes=64)
-            (nc.scalar.copy if j0 in CAST_ON_SCALAR else nc.vector.tensor_copy)(
-                y_bf[:].rearrange("p (g i u) -> p g u i", i=4, u=PACK),
+        def weave_y(y, y_bf, copy):
+            copy(
+                y_bf.rearrange("p (g i u) -> p g u i", i=4, u=PACK),
                 y[:].rearrange("p u (g i) -> p g u i", i=4),
             )
-            nc.vector.quantize_mx(out=y_codes[:, cols].bitcast(FP8X4), scales=y_scales[:, cols], in_=y_bf[:])
+
+        def quantize_y(j0, width, y_bf):
+            quantize(y_codes[:, j0 : j0 + width], y_scales[:, j0 : j0 + width], y_bf)
             if j0 + width in WORD_STORES:
                 done = slice(max(e for e in (0,) + WORD_STORES if e < j0 + width), j0 + width)
                 nc.sync.dma_start(y_words[:, done], y_codes[:, done].bitcast(I32))
 
-        last = CHUNKS - 1
+        def after_sig(k, shape, dtype, name):
+            return keep.tile(shape, dtype, name=name, tag=f"sig{k}", align_bytes=64)
+
         by_sub = [(a, s) for s in range(2) for a in range(PASSES)]
         by_pass = [(a, s) for a in range(PASSES) for s in range(2)]
         units = [(c, a, s) for c in range(CHUNKS) for a, s in (by_sub if c in (0, last) else by_pass)]
         ys = {}
+        steps = 0
+        wd_bf = [keep.tile([P, PASSES * PIECE], BF16, name="wd_first", tag="high", align_bytes=64)[:], stage[0][:]]
+        spare = stage[0][:, :PIECE]
         for unit, (c, a, s) in enumerate(units):
+            if unit in (0, PACK):
+                weave_wd(c, slice(0, G_ROWS[c]), wd_bf[c], cast_on_gpsimd, "m u t")
+            while steps < min(len(units), unit + LEAD, 2 * PACK if unit < PACK else len(units)):
+                gate(steps)
+                steps += 1
+                if steps == S_AT[0]:
+                    weave_wd(0, slice(G_ROWS[0], P), wd_bf[0], nc.scalar.copy, "m t u")
+            if unit == S_AT[1]:
+                weave_wd(1, slice(G_ROWS[1], P), wd_bf[1], nc.scalar.copy, "m t u")
+            if unit == last * PACK:
+                cast_on_gpsimd(spare.rearrange("p (j u) -> p j u", u=PACK), ys[0][:].rearrange("p u j -> p j u"))
             hidden(unit, c, a, s)
-            if unit < 2:
-                if unit == 0:
-                    quantize_x(1, whole)
-                last_plane(2 + unit, whole)
-            elif unit < 4:
-                quantize_x(unit, whole)
-            for wa in range(PASSES):
+            if unit == 3:
+                late_codes, late_scales = mx_tile(2 * CHUNK, "x_late_mx", "sig0")
+                quantize(late_codes, late_scales, x_late[:])
                 for k in range(2):
-                    if WD_AT[wa] + k == unit:
-                        weave_wd(wa, k, nc.scalar.copy if (wa, k) == (1, 1) else nc.vector.tensor_copy)
-            if unit >= 1:
-                pc, pa, ps = units[unit - 1]
-                if pc == last:
-                    quantize_h(pa, pc * CHUNK + ps * SUB, SUB)
-                elif ps == 1:
-                    quantize_h(pa, pc * CHUNK, CHUNK)
+                    x_codes.append(late_codes[:, k * CHUNK : (k + 1) * CHUNK])
+                    x_scales.append(late_scales[:, k * CHUNK : (k + 1) * CHUNK])
+                quantize_h(0, 0, PASSES * CHUNK)
+                quantize_wd(0, wd_bf[0])
+            if unit == 7:
+                quantize_wd(1, wd_bf[1])
+                quantize_h(1, 0, PASSES * CHUNK)
+            if unit == 11:
+                quantize_h(2, 0, CHUNK)
+                quantize_h(2, CHUNK, PASSES * CHUNK)
             for d in range(last):
                 if unit == DOWN_AT[d]:
-                    ys[d] = down(d * CHUNK, CHUNK, y_banks, False)
-            for d, at in enumerate(PLANES_AT):
-                if unit == at:
-                    planes_of(d * CHUNK, CHUNK, ys[d])
+                    ys[d] = down(d * CHUNK, CHUNK, y_banks if d < 2 else gate_banks[:2])
             if unit == len(units) - 2:
-                tail = [gate_banks[(unit - 1) % DEPTH][:, :, :SUB], gate_banks[unit % DEPTH][:, :, :SUB]]
-                ys[last] = down(last * CHUNK, SUB, tail, False)
+                quantize_h(last, 0, CHUNK)
+                ys[last] = down(last * CHUNK, SUB, [bank[:, :, :SUB] for bank in y_banks])
         unit = len(units) - 1
-        quantize_h(PASSES - 1, J - SUB, SUB)
-        tail = [gate_banks[unit % DEPTH][:, :, :SUB], up_banks[(unit - 2) % DEPTH][:, 0:2, :]]
-        y_end = down(J - SUB, SUB, tail, False)
-        for d in range(len(PLANES_AT), last):
-            planes_of(d * CHUNK, CHUNK, ys[d])
-        planes_of(last * CHUNK, SUB, ys[last])
-        planes_of(J - SUB, SUB, y_end)
+        quantize_y(0, CHUNK, spare)
+        quantize_h(last, CHUNK, PASSES * CHUNK)
+        tail = [gate_banks[2][:, :, :SUB], up_banks[(unit - 2) % DEPTH][:, 0:2, :]]
+        ys[last + 1] = down(J - SUB, SUB, tail)
+        pieces = [(CHUNK, CHUNK), (2 * CHUNK, CHUNK), (last * CHUNK, SUB), (J - SUB, SUB)]
+        tags = ["y_free" if 0 in Y_ON_SCALAR else "sig5", "sig6", "sig7", "y_end"]
+        y_bf = [keep.tile([P, w * PACK], BF16, name=f"y_bf{j0}", tag=tags[d], align_bytes=64)[:] for d, (j0, w) in enumerate(pieces)]
+        for d, (j0, width) in enumerate(pieces):
+            weave_y(ys[d + 1], y_bf[d], nc.scalar.copy if d in Y_ON_SCALAR else nc.vector.tensor_copy)
+            if d >= 1:
+                quantize_y(*pieces[d - 1], y_bf[d - 1])
+        quantize_y(*pieces[-1], y_bf[-1])
 
         for q in range(4):
             queue = nc.sync if q % 2 == 0 else nc.scalar

@@ -26,12 +26,13 @@ SUB = 128
 PER_COL = 16
 DEPTH = 3
 PIECE = CHUNK * PACK
-LEAD = 5
+LEAD = 4
 Y_ON_SCALAR = ()
-G_ROWS = (80, 96)
+G_ROWS = (72, 88)
 S_AT = (4, 5)
-DOWN_AT = (8, 12, 15)
-WORD_STORES = (512, 768, 1024)
+SPLIT = (1, 2, 3)
+DOWN_AT = (10, 13, 15)
+WORD_STORES = (256, 768, 1024)
 
 
 def tile_list_sigm_biasP_kernel(
@@ -52,19 +53,17 @@ def tile_list_sigm_biasP_kernel(
         offsets = keep.tile([P, J // PER_COL], U16, name="offsets")
         nc.sync.dma_start(offsets[:], offs)
 
-        raw_scales = []
+        raw_scales = keep.tile([P, R], U8, name="raw_scales", align_bytes=64)
+        nc.vector.memset(raw_scales[:].bitcast(I32), 0)
         warm = keep.tile([P, 8], F32, name="warm")
 
-        def load_scales(w, scales):
-            tag = ("raw_scales0", "plane1")[w]
-            raw_scales.append(keep.tile([P, R], U8, name=f"raw_scales{w}", tag=tag, align_bytes=64))
-            (nc.vector, nc.gpsimd)[w].memset(raw_scales[w][:].bitcast(I32), 0)
+        def load_scales(scales):
             for q in range(4):
                 nc.scalar.dma_start(
-                    raw_scales[w][32 * q : 32 * q + 4, :].bitcast(I32), scales[0, 4 * q : 4 * q + 4, :].bitcast(I32)
+                    raw_scales[32 * q : 32 * q + 4, :].bitcast(I32), scales[0, 4 * q : 4 * q + 4, :].bitcast(I32)
                 )
 
-        load_scales(0, wg_scales)
+        load_scales(wg_scales)
         nc.vector.memset(warm[:, 0:1], 0.0)
         nc.scalar.activation(warm[:, 4:5], warm[:, 0:1], ACT.Sigmoid)
 
@@ -72,11 +71,11 @@ def tile_list_sigm_biasP_kernel(
         weight = keep.tile([P, J], F32, name="weight", align_bytes=64)
         planes = [keep.tile([P, T], F32, name=f"plane{i}", align_bytes=64) for i in range(PACK)]
         x_planes = xT.rearrange("(p i) t -> i p t", i=PACK)
-        raw_words = [keep.tile([P, 2 * R], U8, name=f"raw_words{w}") for w in range(2)]
-        for i in range(PACK - 1):
+        raw_words = [keep.tile([P, 2 * R], U8, name=f"raw_words{w}", align_bytes=64) for w in range(2)]
+        for i in range(PACK):
+            if i == 2:
+                nc.sync.dma_start(raw_words[0][:].bitcast(I32), wg_words[0].bitcast(I32))
             nc.sync.dma_start(planes[i][:], x_planes[i])
-        nc.sync.dma_start(raw_words[0][:].bitcast(I32), wg_words[0].bitcast(I32))
-        nc.sync.dma_start(planes[PACK - 1][:], x_planes[PACK - 1])
         nc.sync.dma_start(raw_words[1][:].bitcast(I32), wu_words[0].bitcast(I32))
 
         wd_raw = [keep.tile([P, PACK, N], F32, name=f"wd_raw{a}") for a in range(PASSES)]
@@ -130,28 +129,31 @@ def tile_list_sigm_biasP_kernel(
         w_words = []
         w_scales = []
 
-        def deal(w):
-            dealt = keep.tile([P, 3 * R], U8, name=f"dealt{w}", tag=("plane2", "x_head")[w], align_bytes=64)
-            w_words.append(dealt[:, : 2 * R])
-            w_scales.append(dealt[:, 2 * R :])
+        def deal_words(w, tag):
+            w_words.append(keep.tile([P, 2 * R], U8, name=f"w_words{w}", tag=tag, align_bytes=64))
             nc.vector.tensor_copy(
-                w_words[w].bitcast(I32).rearrange("p (a t q h) -> p a q t h", t=PACK, q=32, h=2),
+                w_words[w][:].bitcast(I32).rearrange("p (a t q h) -> p a q t h", t=PACK, q=32, h=2),
                 raw_words[w][:].bitcast(I32).rearrange("p (a q t h) -> p a q t h", t=PACK, q=32, h=2),
             )
+
+        def deal_scales(w, tag):
+            w_scales.append(keep.tile([P, R], U8, name=f"w_scales{w}", tag=tag, align_bytes=64))
             nc.vector.tensor_copy(
-                w_scales[w].bitcast(I32).rearrange("p (g t q) -> p g q t", t=PACK, q=32),
-                raw_scales[w][:].bitcast(I32).rearrange("p (g q t) -> p g q t", t=PACK, q=32),
+                w_scales[w][:].bitcast(I32).rearrange("p (g t q) -> p g q t", t=PACK, q=32),
+                raw_scales[:].bitcast(I32).rearrange("p (g q t) -> p g q t", t=PACK, q=32),
             )
 
         whole = slice(0, CHUNK)
-        gather(low[:, 0, :], 0, 0, J)
-        for j0 in range(0, J, half):
-            gather(low[:, 1, j0 : j0 + half], 1, j0, j0 + half)
-        load_scales(1, wu_scales)
+        for i in range(2):
+            for j0 in range(0, J, half):
+                gather(low[:, i, j0 : j0 + half], i, j0, j0 + half)
+            if i == 0:
+                deal_scales(0, "plane0")
+                load_scales(wu_scales)
+        deal_words(0, "w_words0")
         for j0, j1 in x_parts:
             weave_pair(0, j0, j1)
         gather(high[:, 0, :], 2, 0, J)
-        deal(0)
 
         def last_plane(j0, j1):
             gather(high[:, 1, j0:j1], 3, j0, j1)
@@ -169,7 +171,8 @@ def tile_list_sigm_biasP_kernel(
             weave_pair(1, j0, j1)
         quantize_x(*early[0])
         quantize_x(*early[1])
-        deal(1)
+        deal_scales(1, "x_head")
+        deal_words(1, "raw_words0")
         last_plane(half, J)
         quantize_x(*early[2])
         weave_pair(1, half, J, nc.vector.tensor_copy)
@@ -231,16 +234,25 @@ def tile_list_sigm_biasP_kernel(
                     first_stage(bank[:, v, :], 0, g % PASSES, 2 * k + v, g // PASSES, whole)
                 nc.scalar.activation(sigs[g][:, k], bank[:].rearrange("p v j -> p j v"), ACT.Sigmoid)
 
+        def up_bank(unit):
+            if unit < 2 * PACK:
+                bank = (up_banks + y_banks)[unit % (DEPTH + 2)]
+            elif unit == len(units) - 1:
+                bank = gate_banks[2]
+            else:
+                bank = up_banks[(unit - 2 * PACK) % DEPTH]
+            return bank[:].rearrange("p v j -> p (v j)").rearrange("p (t j) -> p t j", t=PACK)
+
         def hidden(unit, c, a, s):
             cols = slice(s * SUB, (s + 1) * SUB)
             sig = sigs[PASSES * c + a]
-            bank = up_banks[unit % DEPTH]
+            bank = up_bank(unit)
             for t in range(PACK):
                 first_stage(bank[:, t, :], 1, a, t, c, cols)
             h0 = h_column(c, a, s) * PACK
             nc.vector.tensor_tensor(
                 stage[c % 2][:, h0 : h0 + SUB * PACK].rearrange("p (j k v) -> p j k v", k=2, v=2),
-                bank[:].rearrange("p (k v) j -> p j k v", v=2),
+                bank.rearrange("p (k v) j -> p j k v", v=2),
                 sig[:, :, cols, :].rearrange("p k j v -> p j k v"),
                 MULT,
             )
@@ -250,12 +262,13 @@ def tile_list_sigm_biasP_kernel(
 
         y_scales = keep.tile([P, J], U8, name="y_scales", align_bytes=64)
         y_codes = keep.tile([P, J], U32, name="y_codes", align_bytes=64)
+        y_tiles = [keep.tile([P, PACK, CHUNK], F32, name=f"y{c}") for c in range(CHUNKS)]
         y_rows = out_0.rearrange("(p u) j -> p u j", u=PACK)
         y_words = out_1[0].rearrange("p j i -> p (j i)").bitcast(I32)
 
         def down(j0, width, banks):
             c, s = divmod(j0 // SUB, 2)
-            y = keep.tile([P, PACK, width], F32, name=f"y{j0}")
+            y = y_tiles[c][:, :, s * SUB : s * SUB + width]
             for k, bank in enumerate(banks):
                 for a in range(PASSES):
                     cols = slice(h_column(c, a, s), h_column(c, a, s) + width)
@@ -272,13 +285,15 @@ def tile_list_sigm_biasP_kernel(
                 for v in range(2):
                     u = 2 * k + v
                     nc.scalar.activation(y[:, u, :], bank[:, v, :], ACT.Identity, bias=bias[:, u : u + 1])
-            nc.sync.dma_start(y_rows[:, :, j0 : j0 + width], y[:])
+                if (j0 + width) % CHUNK == 0 and (c in SPLIT or k == 1):
+                    rows = slice(2 * k, 2 * k + 2) if c in SPLIT else slice(0, PACK)
+                    nc.sync.dma_start(y_rows[:, rows, c * CHUNK : (c + 1) * CHUNK], y_tiles[c][:, rows, :])
             return y
 
         def weave_y(y, y_bf, copy):
             copy(
                 y_bf.rearrange("p (g i u) -> p g u i", i=4, u=PACK),
-                y[:].rearrange("p u (g i) -> p g u i", i=4),
+                y.rearrange("p u (g i) -> p g u i", i=4),
             )
 
         def quantize_y(j0, width, y_bf):
@@ -296,7 +311,7 @@ def tile_list_sigm_biasP_kernel(
         ys = {}
         steps = 0
         wd_bf = [keep.tile([P, PASSES * PIECE], BF16, name="wd_first", tag="high", align_bytes=64)[:], stage[0][:]]
-        spare = stage[0][:, :PIECE]
+        spare = stage[0][:, PIECE:]
         for unit, (c, a, s) in enumerate(units):
             if unit in (0, PACK):
                 weave_wd(c, slice(0, G_ROWS[c]), wd_bf[c], cast_on_gpsimd, "m u t")
@@ -308,7 +323,7 @@ def tile_list_sigm_biasP_kernel(
             if unit == S_AT[1]:
                 weave_wd(1, slice(G_ROWS[1], P), wd_bf[1], nc.scalar.copy, "m t u")
             if unit == last * PACK:
-                cast_on_gpsimd(spare.rearrange("p (j u) -> p j u", u=PACK), ys[0][:].rearrange("p u j -> p j u"))
+                cast_on_gpsimd(spare.rearrange("p (j u) -> p j u", u=PACK), ys[0].rearrange("p u j -> p j u"))
             hidden(unit, c, a, s)
             if unit == 3:
                 late_codes, late_scales = mx_tile(2 * CHUNK, "x_late_mx", "sig0")
@@ -327,13 +342,11 @@ def tile_list_sigm_biasP_kernel(
             for d in range(last):
                 if unit == DOWN_AT[d]:
                     ys[d] = down(d * CHUNK, CHUNK, y_banks if d < 2 else gate_banks[:2])
-            if unit == len(units) - 2:
-                quantize_h(last, 0, CHUNK)
-                ys[last] = down(last * CHUNK, SUB, [bank[:, :, :SUB] for bank in y_banks])
-        unit = len(units) - 1
+        quantize_h(last, 0, CHUNK)
+        ys[last] = down(last * CHUNK, SUB, [bank[:, :, :SUB] for bank in y_banks])
         quantize_y(0, CHUNK, spare)
         quantize_h(last, CHUNK, PASSES * CHUNK)
-        tail = [gate_banks[2][:, :, :SUB], up_banks[(unit - 2) % DEPTH][:, 0:2, :]]
+        tail = [up_banks[k][:, 0:2, :] for k in (1, 2)]
         ys[last + 1] = down(J - SUB, SUB, tail)
         pieces = [(CHUNK, CHUNK), (2 * CHUNK, CHUNK), (last * CHUNK, SUB), (J - SUB, SUB)]
         tags = ["y_free" if 0 in Y_ON_SCALAR else "sig5", "sig6", "sig7", "y_end"]

@@ -28,7 +28,7 @@ DEPTH = 3
 PIECE = CHUNK * PACK
 LEAD = 4
 Y_ON_SCALAR = ()
-G_ROWS = (72, 88)
+G_ROWS = (80, 76)
 S_AT = (4, 5)
 SPLIT = (1, 2, 3)
 DOWN_AT = (10, 13, 15)
@@ -79,7 +79,7 @@ def tile_list_sigm_biasP_kernel(
         nc.sync.dma_start(raw_words[1][:].bitcast(I32), wu_words[0].bitcast(I32))
 
         wd_raw = [keep.tile([P, PACK, N], F32, name=f"wd_raw{a}") for a in range(PASSES)]
-        wd_rows = wd.rearrange("(a q t e) n -> a t q e n", a=PASSES, t=PACK, e=4)
+        wd_rows = wd.rearrange("(a g t e) n -> a t g e n", a=PASSES, t=PACK, e=8)
         for a in range(PASSES):
             for t in range(PACK):
                 nc.sync.dma_start(wd_raw[a][:, t, :], wd_rows[a, t])
@@ -100,16 +100,16 @@ def tile_list_sigm_biasP_kernel(
             nc.vector.transpose(weight[:, i * half : (i + 1) * half], w_spread[i][:])
 
         low = keep.tile([P, 2, J], F32, name="low")
-        high_flat = keep.tile([P, 2 * J], F32, name="high", align_bytes=64)
-        high = high_flat[:].rearrange("p (t j) -> p t j", t=2)
+        high = keep.tile([P, 2 * J + CHUNK], F32, name="high", align_bytes=64)
         x_head = keep.tile([P, PIECE // 2], BF16, name="x_head", align_bytes=64)
         x_second = keep.tile([P, PIECE], BF16, name="x_second", align_bytes=64)
         x_late = keep.tile([P, 2 * PIECE], BF16, name="x_late", align_bytes=64)
         x_parts = {
             (0, SUB): x_head[:],
-            (SUB, CHUNK): high_flat[:, 2 * J - CHUNK :].bitcast(BF16),
+            (SUB, CHUNK): high[:, 2 * J :].bitcast(BF16),
             (CHUNK, 2 * CHUNK): x_second[:],
-            (half, J): x_late[:],
+            (half, half + CHUNK): x_late[:, :PIECE],
+            (half + CHUNK, J): x_late[:, PIECE:],
         }
         x_codes = [keep.tile([P, CHUNK], U32, name=f"x_codes{c}", align_bytes=64)[:] for c in range(2)]
         x_scales = [keep.tile([P, CHUNK], U8, name=f"x_scales{c}", align_bytes=64)[:] for c in range(2)]
@@ -122,9 +122,18 @@ def tile_list_sigm_biasP_kernel(
                 MULT,
             )
 
+        def last_plane_at(j):
+            return J + j + (CHUNK if j >= half else 0)
+
         def weave_pair(pair, j0, j1, copy=nc.scalar.copy):
             dst = x_parts[j0, j1].rearrange("p (j t) -> p j t", t=PACK)[:, :, 2 * pair : 2 * pair + 2]
-            copy(dst, (low, high)[pair][:, :, j0:j1].rearrange("p t j -> p j t"))
+            if pair == 0:
+                src = low[:, :, j0:j1]
+            else:
+                r0, r1 = j0 // CHUNK, last_plane_at(j0) // CHUNK
+                rows = high[:].rearrange("p (r j) -> p r j", j=CHUNK)
+                src = rows[:, r0 : r1 + 1 : r1 - r0, j0 % CHUNK : j0 % CHUNK + j1 - j0]
+            copy(dst, src.rearrange("p t j -> p j t"))
 
         w_words = []
         w_scales = []
@@ -132,15 +141,15 @@ def tile_list_sigm_biasP_kernel(
         def deal_words(w, tag):
             w_words.append(keep.tile([P, 2 * R], U8, name=f"w_words{w}", tag=tag, align_bytes=64))
             nc.vector.tensor_copy(
-                w_words[w][:].bitcast(I32).rearrange("p (a t q h) -> p a q t h", t=PACK, q=32, h=2),
-                raw_words[w][:].bitcast(I32).rearrange("p (a q t h) -> p a q t h", t=PACK, q=32, h=2),
+                w_words[w][:].bitcast(I32).rearrange("p (a t g h) -> p a g t h", t=PACK, g=16, h=4),
+                raw_words[w][:].bitcast(I32).rearrange("p (a g t h) -> p a g t h", t=PACK, g=16, h=4),
             )
 
         def deal_scales(w, tag):
             w_scales.append(keep.tile([P, R], U8, name=f"w_scales{w}", tag=tag, align_bytes=64))
             nc.vector.tensor_copy(
-                w_scales[w][:].bitcast(I32).rearrange("p (g t q) -> p g q t", t=PACK, q=32),
-                raw_scales[:].bitcast(I32).rearrange("p (g q t) -> p g q t", t=PACK, q=32),
+                w_scales[w][:].bitcast(I32).rearrange("p (a t g h) -> p a g t h", t=PACK, g=16, h=2),
+                raw_scales[:].bitcast(I32).rearrange("p (a g t h) -> p a g t h", t=PACK, g=16, h=2),
             )
 
         whole = slice(0, CHUNK)
@@ -153,10 +162,10 @@ def tile_list_sigm_biasP_kernel(
         deal_words(0, "w_words0")
         for j0, j1 in x_parts:
             weave_pair(0, j0, j1)
-        gather(high[:, 0, :], 2, 0, J)
+        gather(high[:, :J], 2, 0, J)
 
         def last_plane(j0, j1):
-            gather(high[:, 1, j0:j1], 3, j0, j1)
+            gather(high[:, last_plane_at(j0) : last_plane_at(j0) + j1 - j0], 3, j0, j1)
 
         def quantize(codes, scales, values):
             nc.vector.quantize_mx(out=codes.bitcast(FP8X4), scales=scales, in_=values)
@@ -175,7 +184,8 @@ def tile_list_sigm_biasP_kernel(
         deal_words(1, "raw_words0")
         last_plane(half, J)
         quantize_x(*early[2])
-        weave_pair(1, half, J, nc.vector.tensor_copy)
+        weave_pair(1, half + CHUNK, J, nc.vector.tensor_copy)
+        weave_pair(1, half, half + CHUNK, nc.vector.tensor_copy)
 
         wd_codes = {}
         wd_scales = {}
@@ -310,7 +320,7 @@ def tile_list_sigm_biasP_kernel(
         units = [(c, a, s) for c in range(CHUNKS) for a, s in (by_sub if c in (0, last) else by_pass)]
         ys = {}
         steps = 0
-        wd_bf = [keep.tile([P, PASSES * PIECE], BF16, name="wd_first", tag="high", align_bytes=64)[:], stage[0][:]]
+        wd_bf = [high[:, J - CHUNK : 2 * J - CHUNK].bitcast(BF16), stage[0][:]]
         spare = stage[0][:, PIECE:]
         for unit, (c, a, s) in enumerate(units):
             if unit in (0, PACK):
@@ -349,7 +359,7 @@ def tile_list_sigm_biasP_kernel(
         tail = [up_banks[k][:, 0:2, :] for k in (1, 2)]
         ys[last + 1] = down(J - SUB, SUB, tail)
         pieces = [(CHUNK, CHUNK), (2 * CHUNK, CHUNK), (last * CHUNK, SUB), (J - SUB, SUB)]
-        tags = ["y_free" if 0 in Y_ON_SCALAR else "sig5", "sig6", "sig7", "y_end"]
+        tags = ["sig6", "sig7", "y_third", "y_end"]
         y_bf = [keep.tile([P, w * PACK], BF16, name=f"y_bf{j0}", tag=tags[d], align_bytes=64)[:] for d, (j0, w) in enumerate(pieces)]
         for d, (j0, width) in enumerate(pieces):
             weave_y(ys[d + 1], y_bf[d], nc.scalar.copy if d in Y_ON_SCALAR else nc.vector.tensor_copy)
@@ -358,5 +368,5 @@ def tile_list_sigm_biasP_kernel(
         quantize_y(*pieces[-1], y_bf[-1])
 
         for q in range(4):
-            queue = nc.sync if q % 2 == 0 else nc.scalar
+            queue = nc.sync if q == 0 else nc.scalar
             queue.dma_start(out_2[0, 4 * q : 4 * q + 4, :].bitcast(I32), y_scales[32 * q : 32 * q + 4, :].bitcast(I32))

@@ -28,9 +28,11 @@ DEPTH = 3
 PIECE = CHUNK * PACK
 LEAD = 4
 Y_ON_SCALAR = ()
-G_ROWS = (80, 76)
+G_ROWS = (96, 96)
 S_AT = (4, 5)
 SPLIT = (1, 2, 3)
+V_FROM = 768
+X_AT = 3
 DOWN_AT = (10, 13, 15)
 WORD_STORES = (256, 768, 1024)
 
@@ -46,7 +48,8 @@ def tile_list_sigm_biasP_kernel(
         up_banks = [psum.tile([P, PACK, SUB], F32, name=f"up{k}") for k in range(DEPTH)]
         y_banks = [psum.tile([P, 2, CHUNK], F32, name=f"y_sum{k}") for k in range(2)]
         sigs = [keep.tile([P, 2, CHUNK, 2], F32, name=f"sig{k}", align_bytes=64) for k in range(CHUNKS * PASSES)]
-        stage = [keep.tile([P, PASSES * PIECE], BF16, name=f"stage{k}", align_bytes=64) for k in range(2)]
+        joint = keep.tile([P, 4 * PIECE], BF16, name="joint", align_bytes=64)
+        stage = [joint[:, : 2 * PIECE], keep.tile([P, 2 * PIECE], BF16, name="stage1", align_bytes=64)[:]]
 
         w_rows = keep.tile([P, 64], F32, name="w_rows", align_bytes=64)
         nc.scalar.dma_start(w_rows[:], wgt[0:P:PER_COL, :].rearrange("g (r c) -> g r c", c=64))
@@ -99,17 +102,16 @@ def tile_list_sigm_biasP_kernel(
         for i in range(2):
             nc.vector.transpose(weight[:, i * half : (i + 1) * half], w_spread[i][:])
 
-        low = keep.tile([P, 2, J], F32, name="low")
-        high = keep.tile([P, 2 * J + CHUNK], F32, name="high", align_bytes=64)
+        picked_flat = keep.tile([P, PACK * J], F32, name="picked", align_bytes=64)
+        picked = picked_flat[:].rearrange("p (t j) -> p t j", t=PACK)
         x_head = keep.tile([P, PIECE // 2], BF16, name="x_head", align_bytes=64)
         x_second = keep.tile([P, PIECE], BF16, name="x_second", align_bytes=64)
-        x_late = keep.tile([P, 2 * PIECE], BF16, name="x_late", align_bytes=64)
+        x_late = joint[:, 2 * PIECE :]
         x_parts = {
             (0, SUB): x_head[:],
-            (SUB, CHUNK): high[:, 2 * J :].bitcast(BF16),
+            (SUB, CHUNK): picked_flat[:, PACK * J - CHUNK - SUB : PACK * J - SUB].bitcast(BF16),
             (CHUNK, 2 * CHUNK): x_second[:],
             (half, half + CHUNK): x_late[:, :PIECE],
-            (half + CHUNK, J): x_late[:, PIECE:],
         }
         x_codes = [keep.tile([P, CHUNK], U32, name=f"x_codes{c}", align_bytes=64)[:] for c in range(2)]
         x_scales = [keep.tile([P, CHUNK], U8, name=f"x_scales{c}", align_bytes=64)[:] for c in range(2)]
@@ -122,18 +124,15 @@ def tile_list_sigm_biasP_kernel(
                 MULT,
             )
 
-        def last_plane_at(j):
-            return J + j + (CHUNK if j >= half else 0)
-
-        def weave_pair(pair, j0, j1, copy=nc.scalar.copy):
+        def weave_pair(pair, j0, j1):
             dst = x_parts[j0, j1].rearrange("p (j t) -> p j t", t=PACK)[:, :, 2 * pair : 2 * pair + 2]
-            if pair == 0:
-                src = low[:, :, j0:j1]
-            else:
-                r0, r1 = j0 // CHUNK, last_plane_at(j0) // CHUNK
-                rows = high[:].rearrange("p (r j) -> p r j", j=CHUNK)
-                src = rows[:, r0 : r1 + 1 : r1 - r0, j0 % CHUNK : j0 % CHUNK + j1 - j0]
-            copy(dst, src.rearrange("p t j -> p j t"))
+            nc.scalar.copy(dst, picked[:, 2 * pair : 2 * pair + 2, j0:j1].rearrange("p t j -> p j t"))
+
+        def weave_rows(dst, src, copy):
+            copy(
+                dst.rearrange("p (g i t) -> p g t i", i=4, t=PACK),
+                src.rearrange("p t (g i) -> p g t i", i=4),
+            )
 
         w_words = []
         w_scales = []
@@ -155,17 +154,18 @@ def tile_list_sigm_biasP_kernel(
         whole = slice(0, CHUNK)
         for i in range(2):
             for j0 in range(0, J, half):
-                gather(low[:, i, j0 : j0 + half], i, j0, j0 + half)
+                gather(picked[:, i, j0 : j0 + half], i, j0, j0 + half)
             if i == 0:
                 deal_scales(0, "plane0")
                 load_scales(wu_scales)
         deal_words(0, "w_words0")
         for j0, j1 in x_parts:
-            weave_pair(0, j0, j1)
-        gather(high[:, :J], 2, 0, J)
+            if j0 < V_FROM:
+                weave_pair(0, j0, j1)
+        gather(picked[:, 2, :], 2, 0, J)
 
         def last_plane(j0, j1):
-            gather(high[:, last_plane_at(j0) : last_plane_at(j0) + j1 - j0], 3, j0, j1)
+            gather(picked[:, 3, j0:j1], 3, j0, j1)
 
         def quantize(codes, scales, values):
             nc.vector.quantize_mx(out=codes.bitcast(FP8X4), scales=scales, in_=values)
@@ -182,10 +182,10 @@ def tile_list_sigm_biasP_kernel(
         quantize_x(*early[1])
         deal_scales(1, "x_head")
         deal_words(1, "raw_words0")
-        last_plane(half, J)
+        last_plane(V_FROM, J)
+        last_plane(half, V_FROM)
         quantize_x(*early[2])
-        weave_pair(1, half + CHUNK, J, nc.vector.tensor_copy)
-        weave_pair(1, half, half + CHUNK, nc.vector.tensor_copy)
+        weave_rows(x_late[:, (V_FROM - half) * PACK :], picked[:, :, V_FROM:], nc.vector.tensor_copy)
 
         wd_codes = {}
         wd_scales = {}
@@ -228,7 +228,7 @@ def tile_list_sigm_biasP_kernel(
             return (s * PASSES + a) * SUB if c == last else a * CHUNK + s * SUB
 
         def gate(step):
-            bank = gate_banks[step % DEPTH]
+            bank = gate_banks[step % DEPTH if step < last * PACK else step % 2]
             if step < PACK:
                 c, a, s = units[step]
                 cols = slice(s * SUB, (s + 1) * SUB)
@@ -247,10 +247,8 @@ def tile_list_sigm_biasP_kernel(
         def up_bank(unit):
             if unit < 2 * PACK:
                 bank = (up_banks + y_banks)[unit % (DEPTH + 2)]
-            elif unit == len(units) - 1:
-                bank = gate_banks[2]
             else:
-                bank = up_banks[(unit - 2 * PACK) % DEPTH]
+                bank = (up_banks + gate_banks[2:])[unit % (DEPTH + 1)]
             return bank[:].rearrange("p v j -> p (v j)").rearrange("p (t j) -> p t j", t=PACK)
 
         def hidden(unit, c, a, s):
@@ -270,7 +268,7 @@ def tile_list_sigm_biasP_kernel(
         def quantize_h(c, c0, c1):
             quantize(h_codes[c][:, c0:c1], h_scales[c][:, c0:c1], stage[c % 2][:, c0 * PACK : c1 * PACK])
 
-        y_scales = keep.tile([P, J], U8, name="y_scales", align_bytes=64)
+        y_scales = keep.tile([P, CHUNK], U8, name="y_scales", align_bytes=64)
         y_codes = keep.tile([P, J], U32, name="y_codes", align_bytes=64)
         y_tiles = [keep.tile([P, PACK, CHUNK], F32, name=f"y{c}") for c in range(CHUNKS)]
         y_rows = out_0.rearrange("(p u) j -> p u j", u=PACK)
@@ -300,14 +298,9 @@ def tile_list_sigm_biasP_kernel(
                     nc.sync.dma_start(y_rows[:, rows, c * CHUNK : (c + 1) * CHUNK], y_tiles[c][:, rows, :])
             return y
 
-        def weave_y(y, y_bf, copy):
-            copy(
-                y_bf.rearrange("p (g i u) -> p g u i", i=4, u=PACK),
-                y.rearrange("p u (g i) -> p g u i", i=4),
-            )
-
         def quantize_y(j0, width, y_bf):
-            quantize(y_codes[:, j0 : j0 + width], y_scales[:, j0 : j0 + width], y_bf)
+            c, s0 = divmod(j0, CHUNK)
+            quantize(y_codes[:, j0 : j0 + width], y_scales[4 * c :, s0 : s0 + width], y_bf)
             if j0 + width in WORD_STORES:
                 done = slice(max(e for e in (0,) + WORD_STORES if e < j0 + width), j0 + width)
                 nc.sync.dma_start(y_words[:, done], y_codes[:, done].bitcast(I32))
@@ -320,7 +313,7 @@ def tile_list_sigm_biasP_kernel(
         units = [(c, a, s) for c in range(CHUNKS) for a, s in (by_sub if c in (0, last) else by_pass)]
         ys = {}
         steps = 0
-        wd_bf = [high[:, J - CHUNK : 2 * J - CHUNK].bitcast(BF16), stage[0][:]]
+        wd_bf = [picked_flat[:, V_FROM : V_FROM + J].bitcast(BF16), joint[:, PIECE : 3 * PIECE]]
         spare = stage[0][:, PIECE:]
         for unit, (c, a, s) in enumerate(units):
             if unit in (0, PACK):
@@ -328,6 +321,8 @@ def tile_list_sigm_biasP_kernel(
             while steps < min(len(units), unit + LEAD, 2 * PACK if unit < PACK else len(units)):
                 gate(steps)
                 steps += 1
+                if steps == X_AT and V_FROM > half:
+                    weave_pair(1, half, V_FROM)
                 if steps == S_AT[0]:
                     weave_wd(0, slice(G_ROWS[0], P), wd_bf[0], nc.scalar.copy, "m t u")
             if unit == S_AT[1]:
@@ -337,7 +332,7 @@ def tile_list_sigm_biasP_kernel(
             hidden(unit, c, a, s)
             if unit == 3:
                 late_codes, late_scales = mx_tile(2 * CHUNK, "x_late_mx", "sig0")
-                quantize(late_codes, late_scales, x_late[:])
+                quantize(late_codes, late_scales, x_late)
                 for k in range(2):
                     x_codes.append(late_codes[:, k * CHUNK : (k + 1) * CHUNK])
                     x_scales.append(late_scales[:, k * CHUNK : (k + 1) * CHUNK])
@@ -356,17 +351,20 @@ def tile_list_sigm_biasP_kernel(
         ys[last] = down(last * CHUNK, SUB, [bank[:, :, :SUB] for bank in y_banks])
         quantize_y(0, CHUNK, spare)
         quantize_h(last, CHUNK, PASSES * CHUNK)
-        tail = [up_banks[k][:, 0:2, :] for k in (1, 2)]
+        tail = [up_banks[k][:, 0:2, :] for k in (0, 1)]
         ys[last + 1] = down(J - SUB, SUB, tail)
         pieces = [(CHUNK, CHUNK), (2 * CHUNK, CHUNK), (last * CHUNK, SUB), (J - SUB, SUB)]
         tags = ["sig6", "sig7", "y_third", "y_end"]
         y_bf = [keep.tile([P, w * PACK], BF16, name=f"y_bf{j0}", tag=tags[d], align_bytes=64)[:] for d, (j0, w) in enumerate(pieces)]
         for d, (j0, width) in enumerate(pieces):
-            weave_y(ys[d + 1], y_bf[d], nc.scalar.copy if d in Y_ON_SCALAR else nc.vector.tensor_copy)
+            weave_rows(y_bf[d], ys[d + 1], nc.scalar.copy if d in Y_ON_SCALAR else nc.vector.tensor_copy)
             if d >= 1:
                 quantize_y(*pieces[d - 1], y_bf[d - 1])
         quantize_y(*pieces[-1], y_bf[-1])
 
         for q in range(4):
             queue = nc.sync if q == 0 else nc.scalar
-            queue.dma_start(out_2[0, 4 * q : 4 * q + 4, :].bitcast(I32), y_scales[32 * q : 32 * q + 4, :].bitcast(I32))
+            queue.dma_start(
+                out_2[0, 4 * q : 4 * q + 4, :].bitcast(I32).rearrange("r (c j) -> c r j", c=CHUNKS),
+                y_scales[32 * q : 32 * q + 16, :].bitcast(I32),
+            )

@@ -22,19 +22,15 @@ PACK = 4
 PASSES = R // (P * PACK)
 CHUNK = 256
 CHUNKS = J // CHUNK
+LAST = CHUNKS - 1
 SUB = 128
-PER_COL = 16
-DEPTH = 3
+HALF = J // 2
 PIECE = CHUNK * PACK
-LEAD = 4
-Y_ON_SCALAR = ()
-G_ROWS = (96, 96)
-S_AT = (4, 5)
-SPLIT = (1, 2, 3)
-V_FROM = 768
-X_AT = 3
-DOWN_AT = (10, 13, 15)
-WORD_STORES = (256, 768, 1024)
+PER_LIST = 16
+RUN = PASSES * CHUNK // SUB
+RING = 3
+GPSIMD_ROWS = (80, 88)
+WORD_STORES = (CHUNK, 3 * CHUNK, J)
 
 
 def tile_list_sigm_biasP_kernel(
@@ -44,41 +40,43 @@ def tile_list_sigm_biasP_kernel(
     with ExitStack() as ctx:
         keep = ctx.enter_context(tc.tile_pool(name="keep", bufs=1))
         psum = ctx.enter_context(tc.psum_pool(name="psum", bufs=1))
-        gate_banks = [psum.tile([P, 2, CHUNK], F32, name=f"gate{k}") for k in range(DEPTH)]
-        up_banks = [psum.tile([P, PACK, SUB], F32, name=f"up{k}") for k in range(DEPTH)]
+        gate_banks = [psum.tile([P, 2, CHUNK], F32, name=f"gate{k}") for k in range(RING)]
+        up_banks = [psum.tile([P, PACK, SUB], F32, name=f"up{k}") for k in range(RING)]
         y_banks = [psum.tile([P, 2, CHUNK], F32, name=f"y_sum{k}") for k in range(2)]
         sigs = [keep.tile([P, 2, CHUNK, 2], F32, name=f"sig{k}", align_bytes=64) for k in range(CHUNKS * PASSES)]
-        joint = keep.tile([P, 4 * PIECE], BF16, name="joint", align_bytes=64)
-        stage = [joint[:, : 2 * PIECE], keep.tile([P, 2 * PIECE], BF16, name="stage1", align_bytes=64)[:]]
+        h_even = keep.tile([P, 3 * PIECE], BF16, name="h_even", align_bytes=64)
+        h_bf = [h_even[:, : 2 * PIECE], keep.tile([P, 2 * PIECE], BF16, name="h_odd", align_bytes=64)[:]]
 
         w_rows = keep.tile([P, 64], F32, name="w_rows", align_bytes=64)
-        nc.scalar.dma_start(w_rows[:], wgt[0:P:PER_COL, :].rearrange("g (r c) -> g r c", c=64))
-        offsets = keep.tile([P, J // PER_COL], U16, name="offsets")
+        nc.scalar.dma_start(w_rows[:], wgt[0:P:PER_LIST, :].rearrange("g (r c) -> g r c", c=64))
+        offsets = keep.tile([P, J // PER_LIST], U16, name="offsets")
         nc.sync.dma_start(offsets[:], offs)
 
-        raw_scales = keep.tile([P, R], U8, name="raw_scales", align_bytes=64)
+        raw_scales = keep.tile([P, 2 * R], U8, name="raw_scales", align_bytes=64)
         nc.vector.memset(raw_scales[:].bitcast(I32), 0)
         warm = keep.tile([P, 8], F32, name="warm")
 
-        def load_scales(scales):
+        def load_scales(w, scales, queue):
             for q in range(4):
-                nc.scalar.dma_start(
-                    raw_scales[32 * q : 32 * q + 4, :].bitcast(I32), scales[0, 4 * q : 4 * q + 4, :].bitcast(I32)
+                queue.dma_start(
+                    raw_scales[32 * q : 32 * q + 4, w * R : (w + 1) * R].bitcast(I32),
+                    scales[0, 4 * q : 4 * q + 4, :].bitcast(I32),
                 )
 
-        load_scales(wg_scales)
+        load_scales(0, wg_scales, nc.scalar)
         nc.vector.memset(warm[:, 0:1], 0.0)
         nc.scalar.activation(warm[:, 4:5], warm[:, 0:1], ACT.Sigmoid)
 
-        half = J // 2
         weight = keep.tile([P, J], F32, name="weight", align_bytes=64)
-        planes = [keep.tile([P, T], F32, name=f"plane{i}", align_bytes=64) for i in range(PACK)]
-        x_planes = xT.rearrange("(p i) t -> i p t", i=PACK)
+        planes = [keep.tile([P, T], F32, name=f"plane{t}", align_bytes=64) for t in range(PACK)]
+        x_planes = xT.rearrange("(p t) j -> t p j", t=PACK)
         raw_words = [keep.tile([P, 2 * R], U8, name=f"raw_words{w}", align_bytes=64) for w in range(2)]
-        for i in range(PACK):
-            if i == 2:
-                nc.sync.dma_start(raw_words[0][:].bitcast(I32), wg_words[0].bitcast(I32))
-            nc.sync.dma_start(planes[i][:], x_planes[i])
+        for t in range(2):
+            nc.sync.dma_start(planes[t][:], x_planes[t])
+        nc.sync.dma_start(raw_words[0][:].bitcast(I32), wg_words[0].bitcast(I32))
+        nc.sync.dma_start(planes[2][:], x_planes[2])
+        load_scales(1, wu_scales, nc.sync)
+        nc.sync.dma_start(planes[3][:], x_planes[3])
         nc.sync.dma_start(raw_words[1][:].bitcast(I32), wu_words[0].bitcast(I32))
 
         wd_raw = [keep.tile([P, PACK, N], F32, name=f"wd_raw{a}") for a in range(PASSES)]
@@ -87,52 +85,58 @@ def tile_list_sigm_biasP_kernel(
             for t in range(PACK):
                 nc.sync.dma_start(wd_raw[a][:, t, :], wd_rows[a, t])
         bias = keep.tile([P, PACK], F32, name="bias")
-        nc.sync.dma_start(bias[:], b.rearrange("(p t) -> p t", t=PACK))
+        nc.sync.dma_start(bias[:], b.rearrange("(p u) -> p u", u=PACK))
 
         w_turned = keep.tile([P, 64], F32, name="w_turned", align_bytes=64)
         for k in range(2):
             nc.vector.transpose(w_turned[:, 32 * k : 32 * (k + 1)], w_rows[:, 32 * k : 32 * (k + 1)])
-        w_spread = [keep.tile([P, half], F32, name=f"w_spread{i}", align_bytes=64) for i in range(2)]
+        w_spread = [keep.tile([P, HALF], F32, name=f"w_spread{i}", align_bytes=64) for i in range(2)]
         for i in range(2):
-            src = w_turned[:].rearrange("p (b h r) -> p r b h", b=2, h=2)[:, 8 * i : 8 * (i + 1)]
+            src = w_turned[:].rearrange("p (c h r) -> p r c h", c=2, h=2)[:, 8 * i : 8 * (i + 1)]
             nc.vector.tensor_copy(
-                w_spread[i][:].rearrange("p (r b h s) -> p r b h s", b=2, h=2, s=PER_COL),
-                src.unsqueeze(4).to_broadcast([P, 8, 2, 2, PER_COL]),
+                w_spread[i][:].rearrange("p (r c h s) -> p r c h s", c=2, h=2, s=PER_LIST),
+                src.unsqueeze(4).to_broadcast([P, 8, 2, 2, PER_LIST]),
             )
         for i in range(2):
-            nc.vector.transpose(weight[:, i * half : (i + 1) * half], w_spread[i][:])
+            nc.vector.transpose(weight[:, i * HALF : (i + 1) * HALF], w_spread[i][:])
 
         picked_flat = keep.tile([P, PACK * J], F32, name="picked", align_bytes=64)
         picked = picked_flat[:].rearrange("p (t j) -> p t j", t=PACK)
         x_head = keep.tile([P, PIECE // 2], BF16, name="x_head", align_bytes=64)
         x_second = keep.tile([P, PIECE], BF16, name="x_second", align_bytes=64)
-        x_late = joint[:, 2 * PIECE :]
-        x_parts = {
+        x_late = keep.tile([P, 2 * PIECE + (PASSES * PIECE - CHUNK)], BF16, name="x_late", align_bytes=64)
+        x_early = {
             (0, SUB): x_head[:],
             (SUB, CHUNK): picked_flat[:, PACK * J - CHUNK - SUB : PACK * J - SUB].bitcast(BF16),
             (CHUNK, 2 * CHUNK): x_second[:],
-            (half, half + CHUNK): x_late[:, :PIECE],
         }
-        x_codes = [keep.tile([P, CHUNK], U32, name=f"x_codes{c}", align_bytes=64)[:] for c in range(2)]
-        x_scales = [keep.tile([P, CHUNK], U8, name=f"x_scales{c}", align_bytes=64)[:] for c in range(2)]
+        x_codes = [keep.tile([P, CHUNK], U32, name=f"x_codes{c}", align_bytes=64) for c in range(CHUNKS)]
+        x_scales = [keep.tile([P, CHUNK], U8, name=f"x_scales{c}", align_bytes=64) for c in range(CHUNKS)]
 
-        def gather(out, i, j0, j1):
+        def gather(t, j0, j1):
             nc.vector.tensor_tensor(
-                out,
-                planes[i][:].indirect(offsets[:, j0 // PER_COL : j1 // PER_COL]),
+                picked[:, t, j0:j1],
+                planes[t][:].indirect(offsets[:, j0 // PER_LIST : j1 // PER_LIST]),
                 weight[:, j0:j1],
                 MULT,
             )
 
         def weave_pair(pair, j0, j1):
-            dst = x_parts[j0, j1].rearrange("p (j t) -> p j t", t=PACK)[:, :, 2 * pair : 2 * pair + 2]
+            dst = x_early[j0, j1].rearrange("p (j t) -> p j t", t=PACK)[:, :, 2 * pair : 2 * pair + 2]
             nc.scalar.copy(dst, picked[:, 2 * pair : 2 * pair + 2, j0:j1].rearrange("p t j -> p j t"))
 
-        def weave_rows(dst, src, copy):
-            copy(
+        def weave_on_vector(dst, rows):
+            nc.vector.tensor_copy(
                 dst.rearrange("p (g i t) -> p g t i", i=4, t=PACK),
-                src.rearrange("p t (g i) -> p g t i", i=4),
+                rows.rearrange("p t (g i) -> p g t i", i=4),
             )
+
+        def quantize(codes, scales, values):
+            nc.vector.quantize_mx(out=codes.bitcast(FP8X4), scales=scales, in_=values)
+
+        def quantize_early(j0, j1):
+            c, cols = j0 // CHUNK, slice(j0 % CHUNK, j0 % CHUNK + j1 - j0)
+            quantize(x_codes[c][:, cols], x_scales[c][:, cols], x_early[j0, j1])
 
         w_words = []
         w_scales = []
@@ -146,71 +150,63 @@ def tile_list_sigm_biasP_kernel(
 
         def deal_scales(w, tag):
             w_scales.append(keep.tile([P, R], U8, name=f"w_scales{w}", tag=tag, align_bytes=64))
+            raw = raw_scales[:, w * R : (w + 1) * R].bitcast(I32)
             nc.vector.tensor_copy(
                 w_scales[w][:].bitcast(I32).rearrange("p (a t g h) -> p a g t h", t=PACK, g=16, h=2),
-                raw_scales[:].bitcast(I32).rearrange("p (a g t h) -> p a g t h", t=PACK, g=16, h=2),
+                raw.rearrange("p (a g t h) -> p a g t h", t=PACK, g=16, h=2),
             )
 
-        whole = slice(0, CHUNK)
-        for i in range(2):
-            for j0 in range(0, J, half):
-                gather(picked[:, i, j0 : j0 + half], i, j0, j0 + half)
-            if i == 0:
-                deal_scales(0, "plane0")
-                load_scales(wu_scales)
+        for t in range(2):
+            for j0 in range(0, J, HALF):
+                gather(t, j0, j0 + HALF)
         deal_words(0, "w_words0")
-        for j0, j1 in x_parts:
-            if j0 < V_FROM:
-                weave_pair(0, j0, j1)
-        gather(picked[:, 2, :], 2, 0, J)
-
-        def last_plane(j0, j1):
-            gather(picked[:, 3, j0:j1], 3, j0, j1)
-
-        def quantize(codes, scales, values):
-            nc.vector.quantize_mx(out=codes.bitcast(FP8X4), scales=scales, in_=values)
-
-        def quantize_x(j0, j1):
-            c, cols = j0 // CHUNK, slice(j0 % CHUNK, j0 % CHUNK + j1 - j0)
-            quantize(x_codes[c][:, cols], x_scales[c][:, cols], x_parts[j0, j1])
-
-        early = list(x_parts)[:3]
-        for j0, j1 in early:
-            last_plane(j0, j1)
+        deal_scales(0, "plane1")
+        for j0, j1 in x_early:
+            weave_pair(0, j0, j1)
+        gather(2, 0, J)
+        for j0, j1 in x_early:
+            gather(3, j0, j1)
             weave_pair(1, j0, j1)
-        quantize_x(*early[0])
-        quantize_x(*early[1])
+        quantize_early(0, SUB)
+        quantize_early(SUB, CHUNK)
         deal_scales(1, "x_head")
         deal_words(1, "raw_words0")
-        last_plane(V_FROM, J)
-        last_plane(half, V_FROM)
-        quantize_x(*early[2])
-        weave_rows(x_late[:, (V_FROM - half) * PACK :], picked[:, :, V_FROM:], nc.vector.tensor_copy)
+        late = (3, 2)
+        for c in late:
+            gather(3, c * CHUNK, (c + 1) * CHUNK)
+        quantize_early(CHUNK, 2 * CHUNK)
+        for c in late:
+            weave_on_vector(x_late[:, (c - 2) * PIECE : (c - 1) * PIECE], picked[:, :, c * CHUNK : (c + 1) * CHUNK])
+        for c in late:
+            quantize(x_codes[c][:], x_scales[c][:], x_late[:, (c - 2) * PIECE : (c - 1) * PIECE])
 
-        wd_codes = {}
-        wd_scales = {}
+        wd_bf = [x_late[:, 2 * PIECE - CHUNK :], h_even[:, PIECE:]]
+        wd_mx = [keep.tile([P, 5 * N], U8, name=f"wd_mx{a}", align_bytes=64) for a in range(PASSES)]
+        wd_codes = [both[:, : 4 * N].bitcast(U32) for both in wd_mx]
+        wd_scales = [both[:, 4 * N :] for both in wd_mx]
 
-        def cast_on_gpsimd(dst, src):
+        def round_on_gpsimd(dst, src):
             nc.gpsimd.tensor_scalar(dst, src, 1.0, 0.0, MULT, ADD)
 
-        def weave_wd(a, rows, dst, cast, walk):
+        def weave_wd(a, rows, cast, walk):
             cast(
-                dst.rearrange("p (u m t) -> p " + walk, u=PACK, t=PACK)[:, rows],
+                wd_bf[a].rearrange("p (u m t) -> p " + walk, u=PACK, t=PACK)[:, rows],
                 wd_raw[a][:].rearrange("p t (m u) -> p " + walk, u=PACK)[:, rows],
             )
 
-        def mx_tile(width, name, tag):
-            both = keep.tile([P, 5 * width], U8, name=name, tag=tag, align_bytes=64)
-            return both[:, : 4 * width].bitcast(U32), both[:, 4 * width :]
+        def weave_wd_on_gpsimd(a):
+            weave_wd(a, slice(0, GPSIMD_ROWS[a]), round_on_gpsimd, "m u t")
 
-        def quantize_wd(a, src):
-            wd_codes[a], wd_scales[a] = mx_tile(N, f"wd_mx{a}", f"wd_mx{a}")
-            quantize(wd_codes[a], wd_scales[a], src)
+        def weave_wd_on_scalar(a):
+            weave_wd(a, slice(GPSIMD_ROWS[a], P), nc.scalar.copy, "m t u")
 
+        by_half = [(a, s) for s in range(2) for a in range(PASSES)]
+        by_pass = [(a, s) for a in range(PASSES) for s in range(2)]
+        units = [(c, a, s) for c in range(CHUNKS) for a, s in (by_half if c == 0 else by_pass)]
         h_codes = [keep.tile([P, PASSES * CHUNK], U32, name=f"h_codes{c}", align_bytes=64) for c in range(CHUNKS)]
         h_scales = [keep.tile([P, PASSES * CHUNK], U8, name=f"h_scales{c}", align_bytes=64) for c in range(CHUNKS)]
 
-        def first_stage(out, w, a, t, c, cols):
+        def first_product(out, w, a, t, c, cols):
             r0 = (a * PACK + t) * P
             nc.tensor.matmul_mx(
                 out=out,
@@ -222,69 +218,61 @@ def tile_list_sigm_biasP_kernel(
                 stop=True,
             )
 
-        last = CHUNKS - 1
-
         def h_column(c, a, s):
-            return (s * PASSES + a) * SUB if c == last else a * CHUNK + s * SUB
+            return (s * PASSES + a) * SUB if c == LAST else a * CHUNK + s * SUB
 
         def gate(step):
-            bank = gate_banks[step % DEPTH if step < last * PACK else step % 2]
-            if step < PACK:
+            bank = gate_banks[step % RING if step < LAST * RUN else step % 2]
+            if step < RUN:
                 c, a, s = units[step]
                 cols = slice(s * SUB, (s + 1) * SUB)
                 quarters = bank[:].rearrange("p v (h j) -> p (v h) j", h=2)
                 for t in range(PACK):
-                    first_stage(quarters[:, t, :], 0, a, t, c, cols)
+                    first_product(quarters[:, t, :], 0, a, t, c, cols)
                 nc.scalar.activation(
                     sigs[a][:, :, cols, :], quarters.rearrange("p (k v) j -> p k j v", v=2), ACT.Sigmoid
                 )
             else:
-                g, k = divmod(step, 2)
+                ca, k = divmod(step, 2)
                 for v in range(2):
-                    first_stage(bank[:, v, :], 0, g % PASSES, 2 * k + v, g // PASSES, whole)
-                nc.scalar.activation(sigs[g][:, k], bank[:].rearrange("p v j -> p j v"), ACT.Sigmoid)
+                    first_product(bank[:, v, :], 0, ca % PASSES, 2 * k + v, ca // PASSES, slice(0, CHUNK))
+                nc.scalar.activation(sigs[ca][:, k], bank[:].rearrange("p v j -> p j v"), ACT.Sigmoid)
 
-        def up_bank(unit):
-            if unit < 2 * PACK:
-                bank = (up_banks + y_banks)[unit % (DEPTH + 2)]
-            else:
-                bank = (up_banks + gate_banks[2:])[unit % (DEPTH + 1)]
-            return bank[:].rearrange("p v j -> p (v j)").rearrange("p (t j) -> p t j", t=PACK)
-
-        def hidden(unit, c, a, s):
+        def hidden(unit):
+            c, a, s = units[unit]
             cols = slice(s * SUB, (s + 1) * SUB)
-            sig = sigs[PASSES * c + a]
-            bank = up_bank(unit)
+            ring = up_banks + (y_banks if c < 2 else gate_banks[2:])
+            bank = ring[unit % len(ring)][:].rearrange("p v j -> p (v j)").rearrange("p (t j) -> p t j", t=PACK)
             for t in range(PACK):
-                first_stage(bank[:, t, :], 1, a, t, c, cols)
+                first_product(bank[:, t, :], 1, a, t, c, cols)
             h0 = h_column(c, a, s) * PACK
             nc.vector.tensor_tensor(
-                stage[c % 2][:, h0 : h0 + SUB * PACK].rearrange("p (j k v) -> p j k v", k=2, v=2),
+                h_bf[c % 2][:, h0 : h0 + SUB * PACK].rearrange("p (j k v) -> p j k v", k=2, v=2),
                 bank.rearrange("p (k v) j -> p j k v", v=2),
-                sig[:, :, cols, :].rearrange("p k j v -> p j k v"),
+                sigs[PASSES * c + a][:, :, cols, :].rearrange("p k j v -> p j k v"),
                 MULT,
             )
 
         def quantize_h(c, c0, c1):
-            quantize(h_codes[c][:, c0:c1], h_scales[c][:, c0:c1], stage[c % 2][:, c0 * PACK : c1 * PACK])
+            quantize(h_codes[c][:, c0:c1], h_scales[c][:, c0:c1], h_bf[c % 2][:, c0 * PACK : c1 * PACK])
 
-        y_scales = keep.tile([P, CHUNK], U8, name="y_scales", align_bytes=64)
+        y_scales = keep.tile([P, J], U8, name="y_scales", align_bytes=64)
         y_codes = keep.tile([P, J], U32, name="y_codes", align_bytes=64)
-        y_tiles = [keep.tile([P, PACK, CHUNK], F32, name=f"y{c}") for c in range(CHUNKS)]
+        ys = [keep.tile([P, PACK, CHUNK], F32, name=f"y{c}") for c in range(CHUNKS)]
         y_rows = out_0.rearrange("(p u) j -> p u j", u=PACK)
-        y_words = out_1[0].rearrange("p j i -> p (j i)").bitcast(I32)
+        y_words = out_1[0].rearrange("p j u -> p (j u)").bitcast(I32)
 
         def down(j0, width, banks):
             c, s = divmod(j0 // SUB, 2)
-            y = y_tiles[c][:, :, s * SUB : s * SUB + width]
             for k, bank in enumerate(banks):
                 for a in range(PASSES):
                     cols = slice(h_column(c, a, s), h_column(c, a, s) + width)
                     for v in range(2):
+                        m = slice((2 * k + v) * P, (2 * k + v + 1) * P)
                         nc.tensor.matmul_mx(
                             out=bank[:, v, :],
-                            lhsT=wd_codes[a][:, (2 * k + v) * P : (2 * k + v + 1) * P].bitcast(FP8X4),
-                            lhsT_scale=wd_scales[a][:, (2 * k + v) * P : (2 * k + v + 1) * P],
+                            lhsT=wd_codes[a][:, m].bitcast(FP8X4),
+                            lhsT_scale=wd_scales[a][:, m],
                             rhs=h_codes[c][:, cols].bitcast(FP8X4),
                             rhs_scale=h_scales[c][:, cols],
                             start=(a == 0 and v == 0),
@@ -292,79 +280,69 @@ def tile_list_sigm_biasP_kernel(
                         )
                 for v in range(2):
                     u = 2 * k + v
-                    nc.scalar.activation(y[:, u, :], bank[:, v, :], ACT.Identity, bias=bias[:, u : u + 1])
-                if (j0 + width) % CHUNK == 0 and (c in SPLIT or k == 1):
-                    rows = slice(2 * k, 2 * k + 2) if c in SPLIT else slice(0, PACK)
-                    nc.sync.dma_start(y_rows[:, rows, c * CHUNK : (c + 1) * CHUNK], y_tiles[c][:, rows, :])
-            return y
+                    nc.scalar.activation(
+                        ys[c][:, u, s * SUB : s * SUB + width], bank[:, v, :], ACT.Identity, bias=bias[:, u : u + 1]
+                    )
+                if (j0 + width) % CHUNK == 0:
+                    rows = slice(2 * k, 2 * k + 2)
+                    nc.sync.dma_start(y_rows[:, rows, c * CHUNK : (c + 1) * CHUNK], ys[c][:, rows, :])
 
-        def quantize_y(j0, width, y_bf):
-            c, s0 = divmod(j0, CHUNK)
-            quantize(y_codes[:, j0 : j0 + width], y_scales[4 * c :, s0 : s0 + width], y_bf)
+        def quantize_y(j0, width, values):
+            quantize(y_codes[:, j0 : j0 + width], y_scales[:, j0 : j0 + width], values)
             if j0 + width in WORD_STORES:
                 done = slice(max(e for e in (0,) + WORD_STORES if e < j0 + width), j0 + width)
                 nc.sync.dma_start(y_words[:, done], y_codes[:, done].bitcast(I32))
 
-        def after_sig(k, shape, dtype, name):
-            return keep.tile(shape, dtype, name=name, tag=f"sig{k}", align_bytes=64)
-
-        by_sub = [(a, s) for s in range(2) for a in range(PASSES)]
-        by_pass = [(a, s) for a in range(PASSES) for s in range(2)]
-        units = [(c, a, s) for c in range(CHUNKS) for a, s in (by_sub if c in (0, last) else by_pass)]
-        ys = {}
+        y_first = h_bf[0][:, PIECE:]
         steps = 0
-        wd_bf = [picked_flat[:, V_FROM : V_FROM + J].bitcast(BF16), joint[:, PIECE : 3 * PIECE]]
-        spare = stage[0][:, PIECE:]
         for unit, (c, a, s) in enumerate(units):
-            if unit in (0, PACK):
-                weave_wd(c, slice(0, G_ROWS[c]), wd_bf[c], cast_on_gpsimd, "m u t")
-            while steps < min(len(units), unit + LEAD, 2 * PACK if unit < PACK else len(units)):
+            place = unit % RUN
+            if place == 0 and c < PASSES:
+                weave_wd_on_gpsimd(c)
+            while steps < min(len(units), unit + RUN):
                 gate(steps)
                 steps += 1
-                if steps == X_AT and V_FROM > half:
-                    weave_pair(1, half, V_FROM)
-                if steps == S_AT[0]:
-                    weave_wd(0, slice(G_ROWS[0], P), wd_bf[0], nc.scalar.copy, "m t u")
-            if unit == S_AT[1]:
-                weave_wd(1, slice(G_ROWS[1], P), wd_bf[1], nc.scalar.copy, "m t u")
-            if unit == last * PACK:
-                cast_on_gpsimd(spare.rearrange("p (j u) -> p j u", u=PACK), ys[0].rearrange("p u j -> p j u"))
-            hidden(unit, c, a, s)
-            if unit == 3:
-                late_codes, late_scales = mx_tile(2 * CHUNK, "x_late_mx", "sig0")
-                quantize(late_codes, late_scales, x_late)
-                for k in range(2):
-                    x_codes.append(late_codes[:, k * CHUNK : (k + 1) * CHUNK])
-                    x_scales.append(late_scales[:, k * CHUNK : (k + 1) * CHUNK])
-                quantize_h(0, 0, PASSES * CHUNK)
-                quantize_wd(0, wd_bf[0])
-            if unit == 7:
-                quantize_wd(1, wd_bf[1])
+                if steps == RUN - 1:
+                    weave_wd_on_scalar(0)
+            if place == 0 and c == 1:
+                weave_wd_on_scalar(1)
+            if place == 0 and c == LAST:
+                round_on_gpsimd(y_first.rearrange("p (j u) -> p j u", u=PACK), ys[0][:].rearrange("p u j -> p j u"))
+            hidden(unit)
+            if place == RUN - 2 and c >= 2:
+                down((c - 2) * CHUNK, CHUNK, y_banks)
+            if place == RUN - 1 and c == 0:
+                quantize_h(0, 0, CHUNK)
+                quantize_h(0, CHUNK, PASSES * CHUNK)
+                quantize(wd_codes[0], wd_scales[0], wd_bf[0])
+            if place == RUN - 1 and c == 1:
+                quantize(wd_codes[1], wd_scales[1], wd_bf[1])
                 quantize_h(1, 0, PASSES * CHUNK)
-            if unit == 11:
+            if place == RUN - 1 and c == 2:
                 quantize_h(2, 0, CHUNK)
                 quantize_h(2, CHUNK, PASSES * CHUNK)
-            for d in range(last):
-                if unit == DOWN_AT[d]:
-                    ys[d] = down(d * CHUNK, CHUNK, y_banks if d < 2 else gate_banks[:2])
-        quantize_h(last, 0, CHUNK)
-        ys[last] = down(last * CHUNK, SUB, [bank[:, :, :SUB] for bank in y_banks])
-        quantize_y(0, CHUNK, spare)
-        quantize_h(last, CHUNK, PASSES * CHUNK)
-        tail = [up_banks[k][:, 0:2, :] for k in (0, 1)]
-        ys[last + 1] = down(J - SUB, SUB, tail)
-        pieces = [(CHUNK, CHUNK), (2 * CHUNK, CHUNK), (last * CHUNK, SUB), (J - SUB, SUB)]
-        tags = ["sig6", "sig7", "y_third", "y_end"]
-        y_bf = [keep.tile([P, w * PACK], BF16, name=f"y_bf{j0}", tag=tags[d], align_bytes=64)[:] for d, (j0, w) in enumerate(pieces)]
-        for d, (j0, width) in enumerate(pieces):
-            weave_rows(y_bf[d], ys[d + 1], nc.scalar.copy if d in Y_ON_SCALAR else nc.vector.tensor_copy)
+
+        down(2 * CHUNK, CHUNK, gate_banks[:2])
+        quantize_h(LAST, 0, CHUNK)
+        down(LAST * CHUNK, SUB, [bank[:, :, :SUB] for bank in y_banks])
+        quantize_y(0, CHUNK, y_first)
+        quantize_h(LAST, CHUNK, PASSES * CHUNK)
+        down(J - SUB, SUB, [bank[:, 0:2, :] for bank in up_banks[:2]])
+
+        y_middle = keep.tile([P, 2 * PIECE], BF16, name="y_middle", tag=f"sig{len(sigs) - 1}", align_bytes=64)
+        y_end = keep.tile([P, PIECE], BF16, name="y_end", align_bytes=64)
+        parts = [
+            (CHUNK, CHUNK, y_middle[:, :PIECE]),
+            (2 * CHUNK, CHUNK, y_middle[:, PIECE:]),
+            (LAST * CHUNK, SUB, y_end[:, : PIECE // 2]),
+            (J - SUB, SUB, y_end[:, PIECE // 2 :]),
+        ]
+        for d, (j0, width, values) in enumerate(parts):
+            weave_on_vector(values, ys[j0 // CHUNK][:, :, j0 % CHUNK : j0 % CHUNK + width])
             if d >= 1:
-                quantize_y(*pieces[d - 1], y_bf[d - 1])
-        quantize_y(*pieces[-1], y_bf[-1])
+                quantize_y(*parts[d - 1])
+        quantize_y(*parts[-1])
 
         for q in range(4):
-            queue = nc.sync if q == 0 else nc.scalar
-            queue.dma_start(
-                out_2[0, 4 * q : 4 * q + 4, :].bitcast(I32).rearrange("r (c j) -> c r j", c=CHUNKS),
-                y_scales[32 * q : 32 * q + 16, :].bitcast(I32),
-            )
+            queue = nc.sync if q % 2 == 0 else nc.scalar
+            queue.dma_start(out_2[0, 4 * q : 4 * q + 4, :].bitcast(I32), y_scales[32 * q : 32 * q + 4, :].bitcast(I32))

@@ -73,10 +73,10 @@ def tile_list_sigm_biasP_kernel(
         raw_words = [keep.tile([P, 2 * R], U8, name=f"raw_words{w}", align_bytes=64) for w in range(2)]
         for t in range(2):
             nc.sync.dma_start(planes[t][:], x_planes[t])
-        nc.sync.dma_start(raw_words[0][:].bitcast(I32), wg_words[0].bitcast(I32))
         nc.sync.dma_start(planes[2][:], x_planes[2])
         load_scales(1, wu_scales, nc.sync)
         nc.sync.dma_start(planes[3][:], x_planes[3])
+        nc.sync.dma_start(raw_words[0][:].bitcast(I32), wg_words[0].bitcast(I32))
         nc.sync.dma_start(raw_words[1][:].bitcast(I32), wu_words[0].bitcast(I32))
 
         wd_raw = [keep.tile([P, PACK, N], F32, name=f"wd_raw{a}") for a in range(PASSES)]
@@ -148,28 +148,27 @@ def tile_list_sigm_biasP_kernel(
                 raw_words[w][:].bitcast(I32).rearrange("p (a g t h) -> p a g t h", t=PACK, g=16, h=4),
             )
 
-        def deal_scales(w, tag):
-            w_scales.append(keep.tile([P, R], U8, name=f"w_scales{w}", tag=tag, align_bytes=64))
-            raw = raw_scales[:, w * R : (w + 1) * R].bitcast(I32)
+        def deal_scales():
+            dealt = keep.tile([P, 2 * R], U8, name="w_scales", align_bytes=64)
+            w_scales.extend([dealt[:, :R], dealt[:, R:]])
             nc.vector.tensor_copy(
-                w_scales[w][:].bitcast(I32).rearrange("p (a t g h) -> p a g t h", t=PACK, g=16, h=2),
-                raw.rearrange("p (a g t h) -> p a g t h", t=PACK, g=16, h=2),
+                dealt[:].bitcast(I32).rearrange("p (a t g h) -> p a g t h", t=PACK, g=16, h=2),
+                raw_scales[:].bitcast(I32).rearrange("p (a g t h) -> p a g t h", t=PACK, g=16, h=2),
             )
 
         for t in range(2):
             for j0 in range(0, J, HALF):
                 gather(t, j0, j0 + HALF)
-        deal_words(0, "w_words0")
-        deal_scales(0, "plane1")
         for j0, j1 in x_early:
             weave_pair(0, j0, j1)
         gather(2, 0, J)
+        deal_scales()
         for j0, j1 in x_early:
             gather(3, j0, j1)
             weave_pair(1, j0, j1)
+        deal_words(0, "w_words0")
         quantize_early(0, SUB)
         quantize_early(SUB, CHUNK)
-        deal_scales(1, "x_head")
         deal_words(1, "raw_words0")
         late = (3, 2)
         for c in late:
@@ -302,7 +301,7 @@ def tile_list_sigm_biasP_kernel(
             while steps < min(len(units), unit + RUN):
                 gate(steps)
                 steps += 1
-                if steps == RUN - 1:
+                if steps == RUN + 1:
                     weave_wd_on_scalar(0)
             if place == 0 and c == 1:
                 weave_wd_on_scalar(1)

@@ -121,9 +121,10 @@ def tile_list_sigm_biasP_kernel(
                 MULT,
             )
 
-        def weave_pair(pair, j0, j1):
-            dst = x_early[j0, j1].rearrange("p (j t) -> p j t", t=PACK)[:, :, 2 * pair : 2 * pair + 2]
-            nc.scalar.copy(dst, picked[:, 2 * pair : 2 * pair + 2, j0:j1].rearrange("p t j -> p j t"))
+        def weave_pair(pair, j0, j1, cast=nc.scalar.copy):
+            values = x_early[j0, j1] if j0 < HALF else x_late[:, (j0 - HALF) * PACK : (j1 - HALF) * PACK]
+            dst = values.rearrange("p (j t) -> p j t", t=PACK)[:, :, 2 * pair : 2 * pair + 2]
+            cast(dst, picked[:, 2 * pair : 2 * pair + 2, j0:j1].rearrange("p t j -> p j t"))
 
         def weave_on_vector(dst, rows):
             nc.vector.tensor_copy(
@@ -161,6 +162,7 @@ def tile_list_sigm_biasP_kernel(
                 gather(t, j0, j0 + HALF)
         for j0, j1 in x_early:
             weave_pair(0, j0, j1)
+        weave_pair(0, HALF, J)
         gather(2, 0, J)
         deal_scales()
         for j0, j1 in x_early:
@@ -175,7 +177,7 @@ def tile_list_sigm_biasP_kernel(
             gather(3, c * CHUNK, (c + 1) * CHUNK)
         quantize_early(CHUNK, 2 * CHUNK)
         for c in late:
-            weave_on_vector(x_late[:, (c - 2) * PIECE : (c - 1) * PIECE], picked[:, :, c * CHUNK : (c + 1) * CHUNK])
+            weave_pair(1, c * CHUNK, (c + 1) * CHUNK, nc.vector.tensor_copy)
         for c in late:
             quantize(x_codes[c][:], x_scales[c][:], x_late[:, (c - 2) * PIECE : (c - 1) * PIECE])
 

@@ -63,7 +63,6 @@ def tile_list_sigm_biasP_kernel(
                     scales[0, 4 * q : 4 * q + 4, :].bitcast(I32),
                 )
 
-        load_scales(0, wg_scales, nc.scalar)
         nc.vector.memset(warm[:, 0:1], 0.0)
         nc.scalar.activation(warm[:, 4:5], warm[:, 0:1], ACT.Sigmoid)
 
@@ -73,6 +72,7 @@ def tile_list_sigm_biasP_kernel(
         raw_words = [keep.tile([P, 2 * R], U8, name=f"raw_words{w}", align_bytes=64) for w in range(2)]
         for t in range(2):
             nc.sync.dma_start(planes[t][:], x_planes[t])
+        load_scales(0, wg_scales, nc.sync)
         nc.sync.dma_start(planes[2][:], x_planes[2])
         load_scales(1, wu_scales, nc.sync)
         nc.sync.dma_start(planes[3][:], x_planes[3])
@@ -152,10 +152,11 @@ def tile_list_sigm_biasP_kernel(
         def deal_scales():
             dealt = keep.tile([P, 2 * R], U8, name="w_scales", align_bytes=64)
             w_scales.extend([dealt[:, :R], dealt[:, R:]])
-            nc.vector.tensor_copy(
-                dealt[:].bitcast(I32).rearrange("p (a t g h) -> p a g t h", t=PACK, g=16, h=2),
-                raw_scales[:].bitcast(I32).rearrange("p (a g t h) -> p a g t h", t=PACK, g=16, h=2),
-            )
+            for w in range(2):
+                nc.scalar.copy(
+                    w_scales[w].bitcast(U32).rearrange("p (a t g h) -> p a g t h", t=PACK, g=16, h=2),
+                    raw_scales[:, w * R : (w + 1) * R].bitcast(U32).rearrange("p (a g t h) -> p a g t h", t=PACK, g=16, h=2),
+                )
 
         for t in range(2):
             for j0 in range(0, J, HALF):

from contextlib import ExitStack

import concourse.mybir as mybir

K, R, N, T, J = 512, 1024, 512, 2048, 1024
FLOPS = 2 * K * R * J * 2 + 2 * R * N * J

F32 = mybir.dt.float32
BF16 = mybir.dt.bfloat16
I32 = mybir.dt.int32
U32 = mybir.dt.uint32
U16 = mybir.dt.uint16
U8 = mybir.dt.uint8
FP8X4 = mybir.dt.float8_e4m3fn_x4
FP4X4 = mybir.dt.float4_e2m1fn_x4
ACT = mybir.ActivationFunctionType
MULT = mybir.AluOpType.mult
ADD = mybir.AluOpType.add

P = 128
PACK = 4
PASSES = R // (P * PACK)
CHUNK = 256
CHUNKS = J // CHUNK
LAST = CHUNKS - 1
SUB = 128
HALF = J // 2
PIECE = CHUNK * PACK
PER_LIST = 16
RUN = PASSES * CHUNK // SUB
RING = 3
GPSIMD_ROWS = (80, 88)
WORD_STORES = (CHUNK, 3 * CHUNK, J)


def tile_list_sigm_biasP_kernel(
    tc, xT, wgt, wg_words, wg_scales, wu_words, wu_scales, wd, b, offs, out_0, out_1, out_2
):
    nc = tc.nc
    with ExitStack() as ctx:
        keep = ctx.enter_context(tc.tile_pool(name="keep", bufs=1))
        psum = ctx.enter_context(tc.psum_pool(name="psum", bufs=1))
        gate_banks = [psum.tile([P, 2, CHUNK], F32, name=f"gate{k}") for k in range(RING)]
        up_banks = [psum.tile([P, PACK, SUB], F32, name=f"up{k}") for k in range(RING)]
        y_banks = [psum.tile([P, 2, CHUNK], F32, name=f"y_sum{k}") for k in range(2)]
        sigs = [keep.tile([P, 2, CHUNK, 2], F32, name=f"sig{k}", align_bytes=64) for k in range(CHUNKS * PASSES)]
        h_even = keep.tile([P, 3 * PIECE], BF16, name="h_even", align_bytes=64)
        h_bf = [h_even[:, : 2 * PIECE], keep.tile([P, 2 * PIECE], BF16, name="h_odd", align_bytes=64)[:]]

        w_rows = keep.tile([P, 64], F32, name="w_rows", align_bytes=64)
        nc.scalar.dma_start(w_rows[:], wgt[0:P:PER_LIST, :].rearrange("g (r c) -> g r c", c=64))
        offsets = keep.tile([P, J // PER_LIST], U16, name="offsets")
        nc.sync.dma_start(offsets[:], offs)

        raw_scales = keep.tile([P, 2 * R], U8, name="raw_scales", align_bytes=64)
        nc.vector.memset(raw_scales[:].bitcast(I32), 0)
        warm = keep.tile([P, 8], F32, name="warm")

        def load_scales(w, scales, queue):
            for q in range(4):
                queue.dma_start(
                    raw_scales[32 * q : 32 * q + 4, w * R : (w + 1) * R].bitcast(I32),
                    scales[0, 4 * q : 4 * q + 4, :].bitcast(I32),
                )

        nc.vector.memset(warm[:, 0:1], 0.0)
        nc.scalar.activation(warm[:, 4:5], warm[:, 0:1], ACT.Sigmoid)

        weight = keep.tile([P, J], F32, name="weight", align_bytes=64)
        planes = [keep.tile([P, T], F32, name=f"plane{t}", align_bytes=64) for t in range(PACK)]
        x_planes = xT.rearrange("(p t) j -> t p j", t=PACK)
        raw_words = [keep.tile([P, 2 * R], U8, name=f"raw_words{w}", align_bytes=64) for w in range(2)]
        for t in range(2):
            nc.sync.dma_start(planes[t][:], x_planes[t])
        load_scales(0, wg_scales, nc.sync)
        nc.sync.dma_start(planes[2][:], x_planes[2])
        load_scales(1, wu_scales, nc.sync)
        nc.sync.dma_start(planes[3][:], x_planes[3])
        nc.sync.dma_start(raw_words[0][:].bitcast(I32), wg_words[0].bitcast(I32))
        nc.sync.dma_start(raw_words[1][:].bitcast(I32), wu_words[0].bitcast(I32))

        wd_raw = [keep.tile([P, PACK, N], F32, name=f"wd_raw{a}") for a in range(PASSES)]
        wd_rows = wd.rearrange("(a g t e) n -> a t g e n", a=PASSES, t=PACK, e=8)
        for a in range(PASSES):
            for t in range(PACK):
                nc.sync.dma_start(wd_raw[a][:, t, :], wd_rows[a, t])
        bias = keep.tile([P, PACK], F32, name="bias")
        nc.sync.dma_start(bias[:], b.rearrange("(p u) -> p u", u=PACK))

        w_turned = keep.tile([P, 64], F32, name="w_turned", align_bytes=64)
        for k in range(2):
            nc.vector.transpose(w_turned[:, 32 * k : 32 * (k + 1)], w_rows[:, 32 * k : 32 * (k + 1)])
        w_spread = [keep.tile([P, HALF], F32, name=f"w_spread{i}", align_bytes=64) for i in range(2)]
        for i in range(2):
            src = w_turned[:].rearrange("p (c h r) -> p r c h", c=2, h=2)[:, 8 * i : 8 * (i + 1)]
            nc.vector.tensor_copy(
                w_spread[i][:].rearrange("p (r c h s) -> p r c h s", c=2, h=2, s=PER_LIST),
                src.unsqueeze(4).to_broadcast([P, 8, 2, 2, PER_LIST]),
            )
        for i in range(2):
            nc.vector.transpose(weight[:, i * HALF : (i + 1) * HALF], w_spread[i][:])

        picked_flat = keep.tile([P, PACK * J], F32, name="picked", align_bytes=64)
        picked = picked_flat[:].rearrange("p (t j) -> p t j", t=PACK)
        x_head = keep.tile([P, PIECE // 2], BF16, name="x_head", align_bytes=64)
        x_second = keep.tile([P, PIECE], BF16, name="x_second", align_bytes=64)
        x_late = keep.tile([P, 2 * PIECE + (PASSES * PIECE - CHUNK)], BF16, name="x_late", align_bytes=64)
        x_early = {
            (0, SUB): x_head[:],
            (SUB, CHUNK): picked_flat[:, PACK * J - CHUNK - SUB : PACK * J - SUB].bitcast(BF16),
            (CHUNK, 2 * CHUNK): x_second[:],
        }
        x_codes = [keep.tile([P, CHUNK], U32, name=f"x_codes{c}", align_bytes=64) for c in range(CHUNKS)]
        x_scales = [keep.tile([P, CHUNK], U8, name=f"x_scales{c}", align_bytes=64) for c in range(CHUNKS)]

        def gather(t, j0, j1):
            nc.vector.tensor_tensor(
                picked[:, t, j0:j1],
                planes[t][:].indirect(offsets[:, j0 // PER_LIST : j1 // PER_LIST]),
                weight[:, j0:j1],
                MULT,
            )

        def weave_pair(pair, j0, j1, cast=nc.scalar.copy):
            values = x_early[j0, j1] if j0 < HALF else x_late[:, (j0 - HALF) * PACK : (j1 - HALF) * PACK]
            dst = values.rearrange("p (j t) -> p j t", t=PACK)[:, :, 2 * pair : 2 * pair + 2]
            cast(dst, picked[:, 2 * pair : 2 * pair + 2, j0:j1].rearrange("p t j -> p j t"))

        def weave_on_vector(dst, rows):
            nc.vector.tensor_copy(
                dst.rearrange("p (g i t) -> p g t i", i=4, t=PACK),
                rows.rearrange("p t (g i) -> p g t i", i=4),
            )

        def quantize(codes, scales, values):
            nc.vector.quantize_mx(out=codes.bitcast(FP8X4), scales=scales, in_=values)

        def quantize_early(j0, j1):
            c, cols = j0 // CHUNK, slice(j0 % CHUNK, j0 % CHUNK + j1 - j0)
            quantize(x_codes[c][:, cols], x_scales[c][:, cols], x_early[j0, j1])

        w_words = []
        w_scales = []

        def deal_words(w, tag):
            w_words.append(keep.tile([P, 2 * R], U8, name=f"w_words{w}", tag=tag, align_bytes=64))
            nc.vector.tensor_copy(
                w_words[w][:].bitcast(I32).rearrange("p (a t g h) -> p a g t h", t=PACK, g=16, h=4),
                raw_words[w][:].bitcast(I32).rearrange("p (a g t h) -> p a g t h", t=PACK, g=16, h=4),
            )

        def deal_scales():
            dealt = keep.tile([P, 2 * R], U8, name="w_scales", align_bytes=64)
            w_scales.extend([dealt[:, :R], dealt[:, R:]])
            for w in range(2):
                nc.scalar.copy(
                    w_scales[w].bitcast(U32).rearrange("p (a t g h) -> p a g t h", t=PACK, g=16, h=2),
                    raw_scales[:, w * R : (w + 1) * R].bitcast(U32).rearrange("p (a g t h) -> p a g t h", t=PACK, g=16, h=2),
                )

        for t in range(2):
            for j0 in range(0, J, HALF):
                gather(t, j0, j0 + HALF)
        for j0, j1 in x_early:
            weave_pair(0, j0, j1)
        weave_pair(0, HALF, J)
        gather(2, 0, J)
        deal_scales()
        for j0, j1 in x_early:
            gather(3, j0, j1)
            weave_pair(1, j0, j1)
        deal_words(0, "w_words0")
        quantize_early(0, SUB)
        quantize_early(SUB, CHUNK)
        deal_words(1, "raw_words0")
        late = (3, 2)
        for c in late:
            gather(3, c * CHUNK, (c + 1) * CHUNK)
        quantize_early(CHUNK, 2 * CHUNK)
        for c in late:
            weave_pair(1, c * CHUNK, (c + 1) * CHUNK, nc.vector.tensor_copy)
        for c in late:
            quantize(x_codes[c][:], x_scales[c][:], x_late[:, (c - 2) * PIECE : (c - 1) * PIECE])

        wd_bf = [x_late[:, 2 * PIECE - CHUNK :], h_even[:, PIECE:]]
        wd_mx = [keep.tile([P, 5 * N], U8, name=f"wd_mx{a}", align_bytes=64) for a in range(PASSES)]
        wd_codes = [both[:, : 4 * N].bitcast(U32) for both in wd_mx]
        wd_scales = [both[:, 4 * N :] for both in wd_mx]

        def round_on_gpsimd(dst, src):
            nc.gpsimd.tensor_scalar(dst, src, 1.0, 0.0, MULT, ADD)

        def weave_wd(a, rows, cast, walk):
            cast(
                wd_bf[a].rearrange("p (u m t) -> p " + walk, u=PACK, t=PACK)[:, rows],
                wd_raw[a][:].rearrange("p t (m u) -> p " + walk, u=PACK)[:, rows],
            )

        def weave_wd_on_gpsimd(a):
            weave_wd(a, slice(0, GPSIMD_ROWS[a]), round_on_gpsimd, "m u t")

        def weave_wd_on_scalar(a):
            weave_wd(a, slice(GPSIMD_ROWS[a], P), nc.scalar.copy, "m t u")

        by_half = [(a, s) for s in range(2) for a in range(PASSES)]
        by_pass = [(a, s) for a in range(PASSES) for s in range(2)]
        units = [(c, a, s) for c in range(CHUNKS) for a, s in (by_half if c == 0 else by_pass)]
        h_codes = [keep.tile([P, PASSES * CHUNK], U32, name=f"h_codes{c}", align_bytes=64) for c in range(CHUNKS)]
        h_scales = [keep.tile([P, PASSES * CHUNK], U8, name=f"h_scales{c}", align_bytes=64) for c in range(CHUNKS)]

        def first_product(out, w, a, t, c, cols):
            r0 = (a * PACK + t) * P
            nc.tensor.matmul_mx(
                out=out,
                lhsT=w_words[w][:, 2 * r0 : 2 * (r0 + P)].bitcast(FP4X4),
                lhsT_scale=w_scales[w][:, r0 : r0 + P],
                rhs=x_codes[c][:, cols].bitcast(FP8X4),
                rhs_scale=x_scales[c][:, cols],
                start=True,
                stop=True,
            )

        def h_column(c, a, s):
            return (s * PASSES + a) * SUB if c == LAST else a * CHUNK + s * SUB

        def gate(step):
            bank = gate_banks[step % RING if step < LAST * RUN else step % 2]
            if step < RUN:
                c, a, s = units[step]
                cols = slice(s * SUB, (s + 1) * SUB)
                quarters = bank[:].rearrange("p v (h j) -> p (v h) j", h=2)
                for t in range(PACK):
                    first_product(quarters[:, t, :], 0, a, t, c, cols)
                nc.scalar.activation(
                    sigs[a][:, :, cols, :], quarters.rearrange("p (k v) j -> p k j v", v=2), ACT.Sigmoid
                )
            else:
                ca, k = divmod(step, 2)
                for v in range(2):
                    first_product(bank[:, v, :], 0, ca % PASSES, 2 * k + v, ca // PASSES, slice(0, CHUNK))
                nc.scalar.activation(sigs[ca][:, k], bank[:].rearrange("p v j -> p j v"), ACT.Sigmoid)

        def hidden(unit):
            c, a, s = units[unit]
            cols = slice(s * SUB, (s + 1) * SUB)
            ring = up_banks + (y_banks if c < 2 else gate_banks[2:])
            bank = ring[unit % len(ring)][:].rearrange("p v j -> p (v j)").rearrange("p (t j) -> p t j", t=PACK)
            for t in range(PACK):
                first_product(bank[:, t, :], 1, a, t, c, cols)
            h0 = h_column(c, a, s) * PACK
            nc.vector.tensor_tensor(
                h_bf[c % 2][:, h0 : h0 + SUB * PACK].rearrange("p (j k v) -> p j k v", k=2, v=2),
                bank.rearrange("p (k v) j -> p j k v", v=2),
                sigs[PASSES * c + a][:, :, cols, :].rearrange("p k j v -> p j k v"),
                MULT,
            )

        def quantize_h(c, c0, c1):
            quantize(h_codes[c][:, c0:c1], h_scales[c][:, c0:c1], h_bf[c % 2][:, c0 * PACK : c1 * PACK])

        y_scales = keep.tile([P, J], U8, name="y_scales", align_bytes=64)
        y_codes = keep.tile([P, J], U32, name="y_codes", align_bytes=64)
        ys = [keep.tile([P, PACK, CHUNK], F32, name=f"y{c}") for c in range(CHUNKS)]
        y_rows = out_0.rearrange("(p u) j -> p u j", u=PACK)
        y_words = out_1[0].rearrange("p j u -> p (j u)").bitcast(I32)

        def down(j0, width, banks):
            c, s = divmod(j0 // SUB, 2)
            for k, bank in enumerate(banks):
                for a in range(PASSES):
                    cols = slice(h_column(c, a, s), h_column(c, a, s) + width)
                    for v in range(2):
                        m = slice((2 * k + v) * P, (2 * k + v + 1) * P)
                        nc.tensor.matmul_mx(
                            out=bank[:, v, :],
                            lhsT=wd_codes[a][:, m].bitcast(FP8X4),
                            lhsT_scale=wd_scales[a][:, m],
                            rhs=h_codes[c][:, cols].bitcast(FP8X4),
                            rhs_scale=h_scales[c][:, cols],
                            start=(a == 0 and v == 0),
                            stop=(a == PASSES - 1 and v == 1),
                        )
                for v in range(2):
                    u = 2 * k + v
                    nc.scalar.activation(
                        ys[c][:, u, s * SUB : s * SUB + width], bank[:, v, :], ACT.Identity, bias=bias[:, u : u + 1]
                    )
                if (j0 + width) % CHUNK == 0:
                    rows = slice(2 * k, 2 * k + 2)
                    nc.sync.dma_start(y_rows[:, rows, c * CHUNK : (c + 1) * CHUNK], ys[c][:, rows, :])

        def quantize_y(j0, width, values):
            quantize(y_codes[:, j0 : j0 + width], y_scales[:, j0 : j0 + width], values)
            if j0 + width in WORD_STORES:
                done = slice(max(e for e in (0,) + WORD_STORES if e < j0 + width), j0 + width)
                nc.sync.dma_start(y_words[:, done], y_codes[:, done].bitcast(I32))

        y_first = h_bf[0][:, PIECE:]
        steps = 0
        for unit, (c, a, s) in enumerate(units):
            place = unit % RUN
            if place == 0 and c < PASSES:
                weave_wd_on_gpsimd(c)
            while steps < min(len(units), unit + RUN):
                gate(steps)
                steps += 1
                if steps == RUN + 1:
                    weave_wd_on_scalar(0)
            if place == 0 and c == 1:
                weave_wd_on_scalar(1)
            if place == 0 and c == LAST:
                round_on_gpsimd(y_first.rearrange("p (j u) -> p j u", u=PACK), ys[0][:].rearrange("p u j -> p j u"))
            hidden(unit)
            if place == RUN - 2 and c >= 2:
                down((c - 2) * CHUNK, CHUNK, y_banks)
            if place == RUN - 1 and c == 0:
                quantize_h(0, 0, CHUNK)
                quantize_h(0, CHUNK, PASSES * CHUNK)
                quantize(wd_codes[0], wd_scales[0], wd_bf[0])
            if place == RUN - 1 and c == 1:
                quantize(wd_codes[1], wd_scales[1], wd_bf[1])
                quantize_h(1, 0, PASSES * CHUNK)
            if place == RUN - 1 and c == 2:
                quantize_h(2, 0, CHUNK)
                quantize_h(2, CHUNK, PASSES * CHUNK)

        down(2 * CHUNK, CHUNK, gate_banks[:2])
        quantize_h(LAST, 0, CHUNK)
        down(LAST * CHUNK, SUB, [bank[:, :, :SUB] for bank in y_banks])
        quantize_y(0, CHUNK, y_first)
        quantize_h(LAST, CHUNK, PASSES * CHUNK)
        down(J - SUB, SUB, [bank[:, 0:2, :] for bank in up_banks[:2]])

        y_middle = keep.tile([P, 2 * PIECE], BF16, name="y_middle", tag=f"sig{len(sigs) - 1}", align_bytes=64)
        y_end = keep.tile([P, PIECE], BF16, name="y_end", align_bytes=64)
        parts = [
            (CHUNK, CHUNK, y_middle[:, :PIECE]),
            (2 * CHUNK, CHUNK, y_middle[:, PIECE:]),
            (LAST * CHUNK, SUB, y_end[:, : PIECE // 2]),
            (J - SUB, SUB, y_end[:, PIECE // 2 :]),
        ]
        for d, (j0, width, values) in enumerate(parts):
            weave_on_vector(values, ys[j0 // CHUNK][:, :, j0 % CHUNK : j0 % CHUNK + width])
            if d >= 1:
                quantize_y(*parts[d - 1])
        quantize_y(*parts[-1])

        for q in range(4):
            queue = nc.sync if q % 2 == 0 else nc.scalar
            queue.dma_start(out_2[0, 4 * q : 4 * q + 4, :].bitcast(I32), y_scales[32 * q : 32 * q + 4, :].bitcast(I32))
